import numpy as np
import ml_dtypes


def mxq(x, axis, fmt="e4m3"):
    dtype, down = {"e4m3": (ml_dtypes.float8_e4m3fn, 7), "e5m2": (ml_dtypes.float8_e5m2, 14)}[fmt]
    v = np.moveaxis(np.asarray(x, np.float32).astype(ml_dtypes.bfloat16).astype(np.float64), axis, -1)
    blocks = v.reshape(v.shape[:-1] + (-1, 32))
    amax = np.abs(blocks).max(-1, keepdims=True)
    byte = np.maximum(np.where(amax > 0, np.frexp(amax)[1] - 1 + 127, 0) - down, 1)
    scale = np.exp2(byte - 127.0)
    codes = (blocks / scale).astype(np.float32).astype(dtype).astype(np.float64)
    return np.moveaxis((codes * scale).reshape(v.shape), -1, axis)


WIDE = False


def mx_kscale(k):
    if not WIDE:
        return np.ones(k)
    levels = np.array([10, -10, 5, -5, 0])
    if k % 512:
        return np.exp2(np.random.permutation(np.resize(levels, k // 32))).repeat(32)
    a = np.empty((k // 512, 16))
    for p in range(k // 512):
        a[p, :8] = np.random.permutation(np.resize(levels, 8))
        for g in range(8):
            far = levels[np.abs(levels - a[p, g]) >= 10]
            a[p, g + 8] = far[np.random.randint(len(far))]
    return np.exp2(a.ravel()).repeat(32)


def f64(x):
    return np.asarray(x).astype(np.float64)


def striped(idx):
    return np.tile(idx.reshape(-1, 16).T, (8, 1)).astype(np.uint16)


def unstriped(offs):
    return offs[:16].T.reshape(-1).astype(np.int64)


E2M1 = np.array([0.0, 0.5, 1.0, 1.5, 2.0, 3.0, 4.0, 6.0, -0.0, -0.5, -1.0, -1.5, -2.0, -3.0, -4.0, -6.0])


def pack_weight(w, fmt):
    k, n = w.shape
    w = f64(np.asarray(w, np.float32).astype(ml_dtypes.bfloat16)).reshape(k // 32, 32, n)
    amax = np.abs(w).max(1)
    if fmt == "e4m3":
        byte = np.frexp(amax)[1] - 1 + 127 - 7
    else:
        mant, ex = np.frexp(amax / 6.0)
        byte = np.where(mant > 0.5, ex, ex - 1) + 127
    byte = np.clip(np.where(amax > 0, byte, 1), 1, 254)
    scaled = (w * np.exp2(127.0 - byte)[:, None, :]).reshape(k, n).astype(np.float32)
    by_word = np.ascontiguousarray(scaled.reshape(k // 512, 128, 4, n).transpose(0, 1, 3, 2))
    if fmt == "e4m3":
        words = by_word.astype(ml_dtypes.float8_e4m3fn).view(np.uint8)
    else:
        c = by_word.astype(ml_dtypes.float4_e2m1fn).view(np.uint8) & 0xF
        words = (c[..., 0::2] | (c[..., 1::2] << 4)).reshape(k // 512, 128, 2 * n)
    return np.ascontiguousarray(words), np.ascontiguousarray(byte.astype(np.uint8).reshape(k // 512, 16, n))


def unpack_weight(words, scales, fmt):
    g, _, n = scales.shape
    words = np.ascontiguousarray(words).reshape(g, 128, n, -1)
    if fmt == "e4m3":
        vals = words.view(ml_dtypes.float8_e4m3fn).astype(np.float64)
    else:
        nib = np.empty((g, 128, n, 4), np.uint8)
        nib[..., 0::2] = words & 0xF
        nib[..., 1::2] = words >> 4
        vals = E2M1[nib]
    vals = vals * np.repeat(np.exp2(scales.astype(np.float64) - 127.0), 8, axis=1)[..., None]
    return vals.transpose(0, 1, 3, 2).reshape(g * 512, n)


def sigmoid(v):
    return 1.0 / (1.0 + np.exp(-np.maximum(v, -700.0)))


K, T, E, C, H, N = 512, 512, 8, 128, 512, 384


def by_expert(wq, xq):
    return np.concatenate([wq[e].T @ xq[:, e * C:(e + 1) * C] for e in range(E)], axis=1)


def setup_inputs():
    n = np.random.standard_normal
    s = mx_kscale(K)[:, None]
    u = mx_kscale(H)
    first = np.random.permutation(np.repeat(np.arange(E), T // E))
    second = (first + 1 + np.random.permutation(np.repeat(np.arange(E - 1), -(-T // (E - 1)))[:T])) % E
    while np.bincount(second, minlength=E).max() != T // E:
        load = np.bincount(second, minlength=E); hi, lo = int(load.argmax()), int(load.argmin())
        t = np.flatnonzero((second == hi) & (first != lo))[0]; second[t] = lo
    slot_token = np.empty(E * C, np.int64); pos = np.empty((2, T), np.int64); fill = np.zeros(E, np.int64)
    place = np.stack([np.random.permutation(C) for _ in range(E)])
    for r, deal in enumerate((first, second)):
        for t in np.random.permutation(T):
            e = deal[t]; j = e * C + place[e, fill[e]]; fill[e] += 1; slot_token[j] = t; pos[r, t] = j
    g = np.random.uniform(0.2, 0.8, T)
    w1 = [pack_weight(m, "e2m1") for m in n((E, K, H)) / np.sqrt(K) / s[None]]
    w3 = [pack_weight(m, "e2m1") for m in n((E, K, H)) / np.sqrt(K) / s[None] * u[None, None, :]]
    w2 = [pack_weight(m, "e2m1") for m in n((E, H, N)) / np.sqrt(H) / u[None, :, None]]
    return {
        "xT": (n((K, T)) * s).astype(np.float32),
        "w1_words": np.stack([m[0] for m in w1]),
        "w1_scales": np.stack([m[1] for m in w1]),
        "w3_words": np.stack([m[0] for m in w3]),
        "w3_scales": np.stack([m[1] for m in w3]),
        "w2_words": np.stack([m[0] for m in w2]),
        "w2_scales": np.stack([m[1] for m in w2]),
        "gate": np.stack([np.tile(g, (N, 1)), np.tile(1.0 - g, (N, 1))]).astype(np.float32),
        "offs": striped(slot_token),
        "pos1": striped(pos[0]),
        "pos2": striped(pos[1]),
    }


def reference(xT, w1_words, w1_scales, w3_words, w3_scales, w2_words, w2_scales, gate, offs, pos1, pos2):
    idx = unstriped(offs)
    w1 = np.stack([unpack_weight(w1_words[e], w1_scales[e], "e2m1") for e in range(E)])
    w3 = np.stack([unpack_weight(w3_words[e], w3_scales[e], "e2m1") for e in range(E)])
    w2 = np.stack([unpack_weight(w2_words[e], w2_scales[e], "e2m1") for e in range(E)])
    xq = mxq(f64(xT)[:, idx], 0, "e4m3")
    h = sigmoid(by_expert(w1, xq))
    h = h * by_expert(w3, xq)
    y = by_expert(w2, mxq(h, 0, "e4m3"))
    return f64(gate[0]) * y[:, unstriped(pos1)] + f64(gate[1]) * y[:, unstriped(pos2)]

@@ -1,0 +1,236 @@
+from contextlib import ExitStack
+
+import concourse.mybir as mybir
+from concourse.masks import make_identity
+
+P = 128
+T, E, C, K, H, N = 512, 8, 128, 512, 512, 384
+NT = N // P
+HALF = T // 2
+FLOPS = 2 * E * C * (2 * K * H + H * N)
+
+F32 = mybir.dt.float32
+BF16 = mybir.dt.bfloat16
+I32 = mybir.dt.int32
+U32 = mybir.dt.uint32
+U16 = mybir.dt.uint16
+U8 = mybir.dt.uint8
+FP8X4 = mybir.dt.float8_e4m3fn_x4
+FP4X4 = mybir.dt.float4_e2m1fn_x4
+MULT = mybir.AluOpType.mult
+ADD = mybir.AluOpType.add
+SIGMOID = mybir.ActivationFunctionType.Sigmoid
+
+X_CHUNKS = ((0, 256), (256, 384), (384, 512))
+Y_ON_VECTOR = {5: 1, 6: 1, 7: 2}
+
+
+def tile_moe_pln_glu_sigmoid_kernel(
+    tc, xT, w1_words, w1_scales, w3_words, w3_scales, w2_words, w2_scales, gate, offs, pos1, pos2, out
+):
+    nc = tc.nc
+    with ExitStack() as ctx:
+        keep = ctx.enter_context(tc.tile_pool(name="keep", bufs=1))
+        work = ctx.enter_context(tc.tile_pool(name="work", bufs=3))
+        psum = ctx.enter_context(tc.psum_pool(name="psum", bufs=2))
+
+        offs_sb = keep.tile([P, E * C // 16], U16, name="offs_sb")
+        pos1_sb = keep.tile([P, T // 16], U16, name="pos1_sb")
+        pos2_sb = keep.tile([P, T // 16], U16, name="pos2_sb")
+
+        x_raw = [keep.tile([P, 4, hi - lo], F32, name=f"x_raw{lo}") for lo, hi in X_CHUNKS]
+        x_grp = [keep.tile([P, hi - lo, 4], BF16, name=f"x_grp{lo}", align_bytes=64) for lo, hi in X_CHUNKS]
+        x_words = keep.tile([P, T], U32, name="x_words", align_bytes=64)
+        x_bytes = keep.tile([P, T], U8, name="x_bytes", align_bytes=64)
+        xv = xT.rearrange("(p j) t -> p j t", j=4)
+        for i, (lo, hi) in enumerate(X_CHUNKS):
+            nc.sync.dma_start(out=x_raw[i][:], in_=xv[:, :, lo:hi])
+        nc.sync.dma_start(offs_sb[:], offs)
+
+        def load_scales(plane, src):
+            for r in range(4):
+                nc.sync.dma_start(
+                    out=plane[r:P:32, :].bitcast(I32).rearrange("q (e n) -> q e n", e=E),
+                    in_=src[:, 0, r:16:4, :].rearrange("e q n -> q e n").bitcast(I32),
+                )
+
+        planes = {}
+        for label, width in (("w1", H), ("w3", H), ("w2", N)):
+            planes[label] = keep.tile([P, E * width], U8, name=f"{label}_sc", align_bytes=64)
+        warm = keep.tile([P, 1], F32, name="warm")
+        nc.vector.memset(warm[:], 0.0)
+        nc.scalar.activation(warm[:], warm[:], SIGMOID)
+        nc.gpsimd.memset(planes["w1"][:].bitcast(I32), 0)
+        nc.vector.memset(planes["w3"][:].bitcast(I32), 0)
+        nc.vector.memset(planes["w2"][:].bitcast(I32), 0)
+        nc.vector.memset(x_bytes[:].bitcast(I32), 0)
+        ident = keep.tile([P, P], F32, name="ident")
+        make_identity(nc, ident[:])
+
+        words_of = {}
+
+        def load_words(label, words, lo, hi):
+            width = words.shape[3]
+            tile = keep.tile([P, (hi - lo) * width], U8, name=f"{label}_{lo}", align_bytes=64)
+            nc.sync.dma_start(
+                out=tile[:].bitcast(I32).rearrange("p (e n) -> p e n", e=hi - lo),
+                in_=words[lo:hi, 0].rearrange("e p n -> p e n").bitcast(I32),
+            )
+            for e in range(lo, hi):
+                words_of[label, e] = tile[:, (e - lo) * width : (e - lo + 1) * width]
+
+        load_scales(planes["w1"], w1_scales)
+        load_words("w1", w1_words, 0, 2)
+        load_words("w3", w3_words, 0, 2)
+        load_scales(planes["w3"], w3_scales)
+        load_words("w1", w1_words, 2, 5)
+        load_words("w3", w3_words, 2, 5)
+        load_words("w2", w2_words, 0, 3)
+        load_scales(planes["w2"], w2_scales)
+        load_words("w1", w1_words, 5, 8)
+        load_words("w3", w3_words, 5, 8)
+        load_words("w2", w2_words, 3, 8)
+        nc.sync.dma_start(pos1_sb[:], pos1)
+        nc.sync.dma_start(pos2_sb[:], pos2)
+        gates = []
+        for g in range(2):
+            gt = keep.tile([P, NT, T], F32, name=f"gate{g}")
+            nc.sync.dma_start(out=gt[:], in_=gate[g].rearrange("(a p) t -> p a t", p=P))
+            gates.append(gt)
+
+        for i, (lo, hi) in enumerate(X_CHUNKS):
+            src = x_raw[i][:].rearrange("p j t -> p t j")
+            split = (hi - lo) * 11 // 16
+            nc.vector.tensor_copy(out=x_grp[i][:, :split, :], in_=src[:, :split, :])
+            nc.scalar.copy(out=x_grp[i][:, split:, :], in_=src[:, split:, :])
+            nc.vector.quantize_mx(
+                out=x_words[:, lo:hi].bitcast(FP8X4),
+                scales=x_bytes[:, lo:hi],
+                in_=x_grp[i][:].rearrange("p t j -> p (t j)"),
+            )
+
+        tok_words, tok_bytes = {}, {}
+
+        def gather(lo, hi):
+            width = (hi - lo) * C
+            gw = keep.tile([P, width], U32, name=f"gw_{lo}", align_bytes=64)
+            gb = keep.tile([P, width], U8, name=f"gb_{lo}", align_bytes=64)
+            part = offs_sb[:, lo * C // 16 : hi * C // 16]
+            nc.vector.tensor_copy(gw[:], x_words[:].indirect(part))
+            nc.vector.tensor_copy(gb[:], x_bytes[:].indirect(part))
+            for e in range(lo, hi):
+                tok_words[e] = gw[:, (e - lo) * C : (e - lo + 1) * C]
+                tok_bytes[e] = gb[:, (e - lo) * C : (e - lo + 1) * C]
+
+        y_sb = [keep.tile([P, E * C], F32, name=f"y_sb{n}") for n in range(NT)]
+        live = {}
+
+        def first_layer(e):
+            a_ps = psum.tile([C, H], F32, name="a_ps")
+            g_ps = psum.tile([C, H], F32, name="g_ps")
+            for ps, label in ((a_ps, "w1"), (g_ps, "w3")):
+                nc.tensor.matmul_mx(
+                    out=ps[:],
+                    lhsT=tok_words[e].bitcast(FP8X4),
+                    lhsT_scale=tok_bytes[e],
+                    rhs=words_of[label, e].bitcast(FP4X4),
+                    rhs_scale=planes[label][:, e * H : (e + 1) * H],
+                    start=True,
+                    stop=True,
+                )
+            sig = work.tile([C, H], F32, name="sig")
+            nc.scalar.activation(sig[:], a_ps[:], SIGMOID)
+            live[e] = (sig, g_ps)
+
+        def product(e):
+            sig, g_ps = live[e]
+            h_row = work.tile([C, H], BF16, name="h_row", align_bytes=64)
+            nc.vector.tensor_tensor(
+                h_row[:].rearrange("c (u m d) -> c u m d", u=2, d=2),
+                sig[:].rearrange("c (m u d) -> c u m d", u=2, d=2),
+                g_ps[:].rearrange("c (m u d) -> c u m d", u=2, d=2),
+                MULT,
+            )
+            live[e] = h_row
+
+        def turn_h(e):
+            h_pairs = live[e][:].bitcast(F32)
+            turn = psum.tile([P, 2, C], F32, name="turn")
+            for u in range(2):
+                nc.tensor.transpose(turn[:, u, :], h_pairs[:, u * P : (u + 1) * P], ident[:])
+            h_grp = work.tile([P, C * 4], BF16, name="h_grp", align_bytes=64)
+            nc.scalar.copy(
+                out=h_grp[:].bitcast(F32).rearrange("p (c u) -> p c u", u=2),
+                in_=turn[:].rearrange("p u c -> p c u"),
+            )
+            live[e] = h_grp
+
+        def quantise_h(e):
+            h_words = work.tile([P, C], U32, name="h_words", align_bytes=64)
+            h_bytes = work.tile([P, C], U8, name="h_bytes", align_bytes=64)
+            nc.vector.quantize_mx(out=h_words[:].bitcast(FP8X4), scales=h_bytes[:], in_=live[e][:])
+            live[e] = (h_words, h_bytes)
+
+        def second_layer(e):
+            h_words, h_bytes = live[e]
+            y_ps = psum.tile([P, N], F32, name="y_ps")
+            for n in range(NT):
+                nc.tensor.matmul_mx(
+                    out=y_ps[:, n * P : (n + 1) * P],
+                    lhsT=words_of["w2", e][:, 2 * P * n : 2 * P * (n + 1)].bitcast(FP4X4),
+                    lhsT_scale=planes["w2"][:, e * N + n * P : e * N + (n + 1) * P],
+                    rhs=h_words[:].bitcast(FP8X4),
+                    rhs_scale=h_bytes[:],
+                    start=True,
+                    stop=True,
+                )
+            live[e] = y_ps
+
+        def keep_y(e):
+            for n in range(NT):
+                copy = nc.vector.tensor_copy if n < Y_ON_VECTOR.get(e, 0) else nc.scalar.copy
+                copy(out=y_sb[n][:, e * C : (e + 1) * C], in_=live[e][:, n * P : (n + 1) * P])
+
+        gathers = {-2: ((0, 1), (1, 2)), 0: ((2, 4),), 2: ((4, 6),), 4: ((6, 8),)}
+        for s in range(-2, E + 3):
+            for lo, hi in gathers.get(s, ()):
+                gather(lo, hi)
+            if 0 <= s < E:
+                product(s)
+            if 0 <= s - 2 < E:
+                quantise_h(s - 2)
+            if 0 <= s - 3 < E:
+                keep_y(s - 3)
+            if 0 <= s + 2 < E:
+                first_layer(s + 2)
+            if 0 <= s < E:
+                turn_h(s)
+            if 0 <= s - 2 < E:
+                second_layer(s - 2)
+
+        parts = {}
+
+        def pick(n, which, lo, hi):
+            if (n, which) not in parts:
+                parts[n, which] = keep.tile([P, T], F32, name=f"part{n}{which}")
+            pos = (pos1_sb, pos2_sb)[which]
+            nc.vector.tensor_tensor(
+                parts[n, which][:, lo:hi], y_sb[n][:].indirect(pos[:, lo // 16 : hi // 16]), gates[which][:, n, lo:hi], MULT
+            )
+
+        def store(n, lo, hi):
+            result = work.tile([P, hi - lo], F32, name=f"result{hi - lo}")
+            nc.vector.tensor_tensor(result[:], parts[n, 0][:, lo:hi], parts[n, 1][:, lo:hi], ADD)
+            nc.sync.dma_start(out=out[n * P : (n + 1) * P, lo:hi], in_=result[:])
+
+        pick(0, 0, 0, T)
+        pick(0, 1, 0, T)
+        for n in range(1, NT):
+            pick(n, 0, 0, T)
+            store(n - 1, 0, T)
+            if n < NT - 1:
+                pick(n, 1, 0, T)
+        pick(NT - 1, 1, 0, HALF)
+        pick(NT - 1, 1, HALF, T)
+        store(NT - 1, 0, HALF)
+        store(NT - 1, HALF, T)

@@ -21,8 +21,9 @@ MULT = mybir.AluOpType.mult
 ADD = mybir.AluOpType.add
 SIGMOID = mybir.ActivationFunctionType.Sigmoid
 
-X_CHUNKS = ((0, 256), (256, 384), (384, 512))
-Y_ON_VECTOR = {5: 1, 6: 1, 7: 2}
+X_CHUNKS = ((0, 256), (256, 512))
+QUAD = 4
+GROUPS = ((0, 2), (2, 4), (4, 6), (6, 7), (7, 8))
 
 
 def tile_moe_pln_glu_sigmoid_kernel(
@@ -32,6 +33,7 @@ def tile_moe_pln_glu_sigmoid_kernel(
     with ExitStack() as ctx:
         keep = ctx.enter_context(tc.tile_pool(name="keep", bufs=1))
         work = ctx.enter_context(tc.tile_pool(name="work", bufs=3))
+        ring = ctx.enter_context(tc.tile_pool(name="ring", bufs=2))
         psum = ctx.enter_context(tc.psum_pool(name="psum", bufs=2))
 
         offs_sb = keep.tile([P, E * C // 16], U16, name="offs_sb")
@@ -45,7 +47,6 @@ def tile_moe_pln_glu_sigmoid_kernel(
         xv = xT.rearrange("(p j) t -> p j t", j=4)
         for i, (lo, hi) in enumerate(X_CHUNKS):
             nc.sync.dma_start(out=x_raw[i][:], in_=xv[:, :, lo:hi])
-        nc.sync.dma_start(offs_sb[:], offs)
 
         def load_scales(plane, src):
             for r in range(4):
@@ -79,24 +80,21 @@ def tile_moe_pln_glu_sigmoid_kernel(
             for e in range(lo, hi):
                 words_of[label, e] = tile[:, (e - lo) * width : (e - lo + 1) * width]
 
-        load_scales(planes["w1"], w1_scales)
         load_words("w1", w1_words, 0, 2)
         load_words("w3", w3_words, 0, 2)
+        load_scales(planes["w1"], w1_scales)
+        nc.sync.dma_start(offs_sb[:], offs)
         load_scales(planes["w3"], w3_scales)
         load_words("w1", w1_words, 2, 5)
         load_words("w3", w3_words, 2, 5)
-        load_words("w2", w2_words, 0, 3)
-        load_scales(planes["w2"], w2_scales)
         load_words("w1", w1_words, 5, 8)
         load_words("w3", w3_words, 5, 8)
-        load_words("w2", w2_words, 3, 8)
+        load_scales(planes["w2"], w2_scales)
+        load_words("w2", w2_words, 0, 8)
         nc.sync.dma_start(pos1_sb[:], pos1)
         nc.sync.dma_start(pos2_sb[:], pos2)
-        gates = []
-        for g in range(2):
-            gt = keep.tile([P, NT, T], F32, name=f"gate{g}")
-            nc.sync.dma_start(out=gt[:], in_=gate[g].rearrange("(a p) t -> p a t", p=P))
-            gates.append(gt)
+        gates = keep.tile([P, 2, T], F32, name="gates")
+        nc.sync.dma_start(out=gates[:], in_=gate[:, :P, :].rearrange("g p t -> p g t"))
 
         for i, (lo, hi) in enumerate(X_CHUNKS):
             src = x_raw[i][:].rearrange("p j t -> p t j")
@@ -111,14 +109,15 @@ def tile_moe_pln_glu_sigmoid_kernel(
 
         tok_words, tok_bytes = {}, {}
 
-        def gather(lo, hi):
-            width = (hi - lo) * C
-            gw = keep.tile([P, width], U32, name=f"gw_{lo}", align_bytes=64)
-            gb = keep.tile([P, width], U8, name=f"gb_{lo}", align_bytes=64)
-            part = offs_sb[:, lo * C // 16 : hi * C // 16]
-            nc.vector.tensor_copy(gw[:], x_words[:].indirect(part))
-            nc.vector.tensor_copy(gb[:], x_bytes[:].indirect(part))
-            for e in range(lo, hi):
+        def gather(lo, cuts):
+            gw = ring.tile([P, 2 * C], U32, name="gw", align_bytes=64)
+            gb = ring.tile([P, 2 * C], U8, name="gb", align_bytes=64)
+            width = 2 * C // cuts
+            for at in range(0, 2 * C, width):
+                part = offs_sb[:, (lo * C + at) // 16 : (lo * C + at + width) // 16]
+                nc.vector.tensor_copy(gw[:, at : at + width], x_words[:].indirect(part))
+                nc.vector.tensor_copy(gb[:, at : at + width], x_bytes[:].indirect(part))
+            for e in range(lo, lo + 2):
                 tok_words[e] = gw[:, (e - lo) * C : (e - lo + 1) * C]
                 tok_bytes[e] = gb[:, (e - lo) * C : (e - lo + 1) * C]
 
@@ -139,7 +138,11 @@ def tile_moe_pln_glu_sigmoid_kernel(
                     stop=True,
                 )
             sig = work.tile([C, H], F32, name="sig")
-            nc.scalar.activation(sig[:], a_ps[:], SIGMOID)
+            nc.scalar.activation(
+                sig[:].rearrange("c (u m d) -> c u m d", u=2, d=2),
+                a_ps[:].rearrange("c (m u d) -> c u m d", u=2, d=2),
+                SIGMOID,
+            )
             live[e] = (sig, g_ps)
 
         def product(e):
@@ -147,66 +150,70 @@ def tile_moe_pln_glu_sigmoid_kernel(
             h_row = work.tile([C, H], BF16, name="h_row", align_bytes=64)
             nc.vector.tensor_tensor(
                 h_row[:].rearrange("c (u m d) -> c u m d", u=2, d=2),
-                sig[:].rearrange("c (m u d) -> c u m d", u=2, d=2),
+                sig[:].rearrange("c (u m d) -> c u m d", u=2, d=2),
                 g_ps[:].rearrange("c (m u d) -> c u m d", u=2, d=2),
                 MULT,
             )
             live[e] = h_row
 
-        def turn_h(e):
-            h_pairs = live[e][:].bitcast(F32)
-            turn = psum.tile([P, 2, C], F32, name="turn")
-            for u in range(2):
-                nc.tensor.transpose(turn[:, u, :], h_pairs[:, u * P : (u + 1) * P], ident[:])
-            h_grp = work.tile([P, C * 4], BF16, name="h_grp", align_bytes=64)
+        def turn_h(lo, hi):
+            turn = psum.tile([P, hi - lo, 2, C], F32, name="turn")
+            for e in range(lo, hi):
+                h_pairs = live[e][:].bitcast(F32)
+                for u in range(2):
+                    nc.tensor.transpose(turn[:, e - lo, u, :], h_pairs[:, u * P : (u + 1) * P], ident[:])
+            h_grp = ring.tile([P, (hi - lo) * C * 4], BF16, name="h_grp", align_bytes=64)
             nc.scalar.copy(
-                out=h_grp[:].bitcast(F32).rearrange("p (c u) -> p c u", u=2),
-                in_=turn[:].rearrange("p u c -> p c u"),
+                out=h_grp[:].bitcast(F32).rearrange("p (e c u) -> p e c u", u=2, c=C),
+                in_=turn[:].rearrange("p e u c -> p e c u"),
             )
-            live[e] = h_grp
+            live[lo, hi] = h_grp
 
-        def quantise_h(e):
-            h_words = work.tile([P, C], U32, name="h_words", align_bytes=64)
-            h_bytes = work.tile([P, C], U8, name="h_bytes", align_bytes=64)
-            nc.vector.quantize_mx(out=h_words[:].bitcast(FP8X4), scales=h_bytes[:], in_=live[e][:])
-            live[e] = (h_words, h_bytes)
+        h_words, h_bytes = {}, {}
 
-        def second_layer(e):
-            h_words, h_bytes = live[e]
-            y_ps = psum.tile([P, N], F32, name="y_ps")
-            for n in range(NT):
+        def quantise_h(lo, hi):
+            words = keep.tile([P, (hi - lo) * C], U32, name=f"h_words{lo}", align_bytes=64)
+            scales = keep.tile([P, (hi - lo) * C], U8, name=f"h_bytes{lo}", align_bytes=64)
+            nc.vector.quantize_mx(out=words[:].bitcast(FP8X4), scales=scales[:], in_=live[lo, hi][:])
+            for e in range(lo, hi):
+                h_words[e] = words[:, (e - lo) * C : (e - lo + 1) * C]
+                h_bytes[e] = scales[:, (e - lo) * C : (e - lo + 1) * C]
+
+        def second_layer(n, lo, tag, copy):
+            y_ps = psum.tile([P, QUAD * C], F32, name=tag)
+            for e in range(lo, lo + QUAD):
                 nc.tensor.matmul_mx(
-                    out=y_ps[:, n * P : (n + 1) * P],
+                    out=y_ps[:, (e - lo) * C : (e - lo + 1) * C],
                     lhsT=words_of["w2", e][:, 2 * P * n : 2 * P * (n + 1)].bitcast(FP4X4),
                     lhsT_scale=planes["w2"][:, e * N + n * P : e * N + (n + 1) * P],
-                    rhs=h_words[:].bitcast(FP8X4),
-                    rhs_scale=h_bytes[:],
+                    rhs=h_words[e].bitcast(FP8X4),
+                    rhs_scale=h_bytes[e],
                     start=True,
                     stop=True,
                 )
-            live[e] = y_ps
+            copy(out=y_sb[n][:, lo * C : (lo + QUAD) * C], in_=y_ps[:])
 
-        def keep_y(e):
-            for n in range(NT):
-                copy = nc.vector.tensor_copy if n < Y_ON_VECTOR.get(e, 0) else nc.scalar.copy
-                copy(out=y_sb[n][:, e * C : (e + 1) * C], in_=live[e][:, n * P : (n + 1) * P])
-
-        gathers = {-2: ((0, 1), (1, 2)), 0: ((2, 4),), 2: ((4, 6),), 4: ((6, 8),)}
-        for s in range(-2, E + 3):
-            for lo, hi in gathers.get(s, ()):
-                gather(lo, hi)
-            if 0 <= s < E:
+        ends_at = {hi - 1: (lo, hi) for lo, hi in GROUPS}
+        gather(0, 2)
+        gather(2, 1)
+        first_layer(0)
+        first_layer(1)
+        for s in range(E + 1):
+            if s < E:
                 product(s)
-            if 0 <= s - 2 < E:
-                quantise_h(s - 2)
-            if 0 <= s - 3 < E:
-                keep_y(s - 3)
-            if 0 <= s + 2 < E:
+            if s + 2 < E:
                 first_layer(s + 2)
-            if 0 <= s < E:
-                turn_h(s)
-            if 0 <= s - 2 < E:
-                second_layer(s - 2)
+            if s - 1 in ends_at:
+                quantise_h(*ends_at[s - 1])
+            if s in ends_at:
+                turn_h(*ends_at[s])
+            if s % 2 == 1 and s + 3 < E:
+                gather(s + 3, 1)
+        second_layer(0, 0, "y_ps", nc.scalar.copy)
+        second_layer(0, QUAD, "y_ps", nc.vector.tensor_copy)
+        for n, tag in ((1, "a_ps"), (2, "g_ps")):
+            for lo in (0, QUAD):
+                second_layer(n, lo, tag, nc.scalar.copy)
 
         parts = {}
 
@@ -215,7 +222,7 @@ def tile_moe_pln_glu_sigmoid_kernel(
                 parts[n, which] = keep.tile([P, T], F32, name=f"part{n}{which}")
             pos = (pos1_sb, pos2_sb)[which]
             nc.vector.tensor_tensor(
-                parts[n, which][:, lo:hi], y_sb[n][:].indirect(pos[:, lo // 16 : hi // 16]), gates[which][:, n, lo:hi], MULT
+                parts[n, which][:, lo:hi], y_sb[n][:].indirect(pos[:, lo // 16 : hi // 16]), gates[:, which, lo:hi], MULT
             )
 
         def store(n, lo, hi):
@@ -223,13 +230,33 @@ def tile_moe_pln_glu_sigmoid_kernel(
             nc.vector.tensor_tensor(result[:], parts[n, 0][:, lo:hi], parts[n, 1][:, lo:hi], ADD)
             nc.sync.dma_start(out=out[n * P : (n + 1) * P, lo:hi], in_=result[:])
 
-        pick(0, 0, 0, T)
-        pick(0, 1, 0, T)
-        for n in range(1, NT):
+        def add_on_tensor(n, lo, hi):
+            by_token = psum.tile([P, hi - lo], F32, name="turn")
+            for at in range(0, hi - lo, P):
+                for which in range(2):
+                    nc.tensor.matmul(
+                        by_token[:, at : at + P],
+                        lhsT=parts[n, which][:, lo + at : lo + at + P],
+                        rhs=ident[:],
+                        is_transpose=True,
+                        start=which == 0,
+                        stop=which == 1,
+                    )
+            summed = work.tile([P, hi - lo], F32, name="sig")
+            nc.scalar.copy(out=summed[:], in_=by_token[:])
+            by_row = psum.tile([P, hi - lo], F32, name="y_ps")
+            for at in range(0, hi - lo, P):
+                nc.tensor.transpose(by_row[:, at : at + P], summed[:, at : at + P], ident[:])
+            result = work.tile([P, hi - lo], F32, name="turned_back")
+            nc.scalar.copy(out=result[:], in_=by_row[:])
+            nc.sync.dma_start(out=out[n * P : (n + 1) * P, lo:hi], in_=result[:])
+
+        for n in range(NT - 1):
             pick(n, 0, 0, T)
-            store(n - 1, 0, T)
-            if n < NT - 1:
-                pick(n, 1, 0, T)
+            pick(n, 1, 0, T)
+            add_on_tensor(n, 0, HALF)
+            add_on_tensor(n, HALF, T)
+        pick(NT - 1, 0, 0, T)
         pick(NT - 1, 1, 0, HALF)
         pick(NT - 1, 1, HALF, T)
         store(NT - 1, 0, HALF)

@@ -21,7 +21,7 @@ MULT = mybir.AluOpType.mult
 ADD = mybir.AluOpType.add
 SIGMOID = mybir.ActivationFunctionType.Sigmoid
 
-X_CHUNKS = ((0, 256), (256, 512))
+X_CHUNKS = ((0, 256), (256, 384), (384, 512))
 QUAD = 4
 GROUPS = ((0, 2), (2, 4), (4, 6), (6, 7), (7, 8))
 
@@ -47,6 +47,7 @@ def tile_moe_pln_glu_sigmoid_kernel(
         xv = xT.rearrange("(p j) t -> p j t", j=4)
         for i, (lo, hi) in enumerate(X_CHUNKS):
             nc.sync.dma_start(out=x_raw[i][:], in_=xv[:, :, lo:hi])
+        nc.sync.dma_start(offs_sb[:], offs)
 
         def load_scales(plane, src):
             for r in range(4):
@@ -80,10 +81,9 @@ def tile_moe_pln_glu_sigmoid_kernel(
             for e in range(lo, hi):
                 words_of[label, e] = tile[:, (e - lo) * width : (e - lo + 1) * width]
 
+        load_scales(planes["w1"], w1_scales)
         load_words("w1", w1_words, 0, 2)
         load_words("w3", w3_words, 0, 2)
-        load_scales(planes["w1"], w1_scales)
-        nc.sync.dma_start(offs_sb[:], offs)
         load_scales(planes["w3"], w3_scales)
         load_words("w1", w1_words, 2, 5)
         load_words("w3", w3_words, 2, 5)
@@ -179,9 +179,9 @@ def tile_moe_pln_glu_sigmoid_kernel(
                 h_words[e] = words[:, (e - lo) * C : (e - lo + 1) * C]
                 h_bytes[e] = scales[:, (e - lo) * C : (e - lo + 1) * C]
 
-        def second_layer(n, lo, tag, copy):
-            y_ps = psum.tile([P, QUAD * C], F32, name=tag)
-            for e in range(lo, lo + QUAD):
+        def second_layer(n, lo, hi, tag, copy):
+            y_ps = psum.tile([P, (hi - lo) * C], F32, name=tag)
+            for e in range(lo, hi):
                 nc.tensor.matmul_mx(
                     out=y_ps[:, (e - lo) * C : (e - lo + 1) * C],
                     lhsT=words_of["w2", e][:, 2 * P * n : 2 * P * (n + 1)].bitcast(FP4X4),
@@ -191,7 +191,7 @@ def tile_moe_pln_glu_sigmoid_kernel(
                     start=True,
                     stop=True,
                 )
-            copy(out=y_sb[n][:, lo * C : (lo + QUAD) * C], in_=y_ps[:])
+            copy(out=y_sb[n][:, lo * C : hi * C], in_=y_ps[:])
 
         ends_at = {hi - 1: (lo, hi) for lo, hi in GROUPS}
         gather(0, 2)
@@ -209,11 +209,12 @@ def tile_moe_pln_glu_sigmoid_kernel(
                 turn_h(*ends_at[s])
             if s % 2 == 1 and s + 3 < E:
                 gather(s + 3, 1)
-        second_layer(0, 0, "y_ps", nc.scalar.copy)
-        second_layer(0, QUAD, "y_ps", nc.vector.tensor_copy)
+        second_layer(0, 0, QUAD, "y_ps", nc.scalar.copy)
+        second_layer(0, QUAD, E - 1, "y_ps", nc.vector.tensor_copy)
+        second_layer(0, E - 1, E, "turn", nc.vector.tensor_copy)
         for n, tag in ((1, "a_ps"), (2, "g_ps")):
             for lo in (0, QUAD):
-                second_layer(n, lo, tag, nc.scalar.copy)
+                second_layer(n, lo, lo + QUAD, tag, nc.scalar.copy)
 
         parts = {}
 
@@ -251,11 +252,14 @@ def tile_moe_pln_glu_sigmoid_kernel(
             nc.scalar.copy(out=result[:], in_=by_row[:])
             nc.sync.dma_start(out=out[n * P : (n + 1) * P, lo:hi], in_=result[:])
 
-        for n in range(NT - 1):
-            pick(n, 0, 0, T)
-            pick(n, 1, 0, T)
-            add_on_tensor(n, 0, HALF)
-            add_on_tensor(n, HALF, T)
+        pick(0, 0, 0, T)
+        pick(0, 1, 0, T)
+        add_on_tensor(0, 0, HALF)
+        add_on_tensor(0, HALF, T)
+        for lo in (0, HALF):
+            pick(1, 0, lo, lo + HALF)
+            pick(1, 1, lo, lo + HALF)
+            add_on_tensor(1, lo, lo + HALF)
         pick(NT - 1, 0, 0, T)
         pick(NT - 1, 1, 0, HALF)
         pick(NT - 1, 1, HALF, T)

@@ -59,13 +59,10 @@ def tile_moe_pln_glu_sigmoid_kernel(
         planes = {}
         for label, width in (("w1", H), ("w3", H), ("w2", N)):
             planes[label] = keep.tile([P, E * width], U8, name=f"{label}_sc", align_bytes=64)
-        warm = keep.tile([P, 1], F32, name="warm")
-        nc.vector.memset(warm[:], 0.0)
-        nc.scalar.activation(warm[:], warm[:], SIGMOID)
-        nc.gpsimd.memset(planes["w1"][:].bitcast(I32), 0)
+        nc.vector.memset(planes["w1"][:].bitcast(I32), 0)
         nc.vector.memset(planes["w3"][:].bitcast(I32), 0)
-        nc.vector.memset(planes["w2"][:].bitcast(I32), 0)
         nc.vector.memset(x_bytes[:].bitcast(I32), 0)
+        nc.vector.memset(planes["w2"][:].bitcast(I32), 0)
         ident = keep.tile([P, P], F32, name="ident")
         make_identity(nc, ident[:])
 
@@ -98,7 +95,7 @@ def tile_moe_pln_glu_sigmoid_kernel(
 
         for i, (lo, hi) in enumerate(X_CHUNKS):
             src = x_raw[i][:].rearrange("p j t -> p t j")
-            split = (hi - lo) * 11 // 16
+            split = (hi - lo) // 2
             nc.vector.tensor_copy(out=x_grp[i][:, :split, :], in_=src[:, :split, :])
             nc.scalar.copy(out=x_grp[i][:, split:, :], in_=src[:, split:, :])
             nc.vector.quantize_mx(
@@ -110,8 +107,8 @@ def tile_moe_pln_glu_sigmoid_kernel(
         tok_words, tok_bytes = {}, {}
 
         def gather(lo, cuts):
-            gw = ring.tile([P, 2 * C], U32, name="gw", align_bytes=64)
-            gb = ring.tile([P, 2 * C], U8, name="gb", align_bytes=64)
+            gw = work.tile([P, 2 * C], U32, name="gw", align_bytes=64)
+            gb = work.tile([P, 2 * C], U8, name="gb", align_bytes=64)
             width = 2 * C // cuts
             for at in range(0, 2 * C, width):
                 part = offs_sb[:, (lo * C + at) // 16 : (lo * C + at + width) // 16]
@@ -137,7 +134,7 @@ def tile_moe_pln_glu_sigmoid_kernel(
                     start=True,
                     stop=True,
                 )
-            sig = work.tile([C, H], F32, name="sig")
+            sig = keep.tile([C, H], F32, name=f"sig{e}")
             nc.scalar.activation(
                 sig[:].rearrange("c (u m d) -> c u m d", u=2, d=2),
                 a_ps[:].rearrange("c (m u d) -> c u m d", u=2, d=2),
@@ -243,7 +240,7 @@ def tile_moe_pln_glu_sigmoid_kernel(
                         start=which == 0,
                         stop=which == 1,
                     )
-            summed = work.tile([P, hi - lo], F32, name="sig")
+            summed = work.tile([P, hi - lo], F32, name="summed")
             nc.scalar.copy(out=summed[:], in_=by_token[:])
             by_row = psum.tile([P, hi - lo], F32, name="y_ps")
             for at in range(0, hi - lo, P):
@@ -252,14 +249,11 @@ def tile_moe_pln_glu_sigmoid_kernel(
             nc.scalar.copy(out=result[:], in_=by_row[:])
             nc.sync.dma_start(out=out[n * P : (n + 1) * P, lo:hi], in_=result[:])
 
-        pick(0, 0, 0, T)
-        pick(0, 1, 0, T)
-        add_on_tensor(0, 0, HALF)
-        add_on_tensor(0, HALF, T)
-        for lo in (0, HALF):
-            pick(1, 0, lo, lo + HALF)
-            pick(1, 1, lo, lo + HALF)
-            add_on_tensor(1, lo, lo + HALF)
+        for n in range(NT - 1):
+            for lo in (0, HALF):
+                pick(n, 0, lo, lo + HALF)
+                pick(n, 1, lo, lo + HALF)
+                add_on_tensor(n, lo, lo + HALF)
         pick(NT - 1, 0, 0, T)
         pick(NT - 1, 1, 0, HALF)
         pick(NT - 1, 1, HALF, T)

@@ -23,6 +23,7 @@ SIGMOID = mybir.ActivationFunctionType.Sigmoid
 
 X_CHUNKS = ((0, 256), (256, 384), (384, 512))
 QUAD = 4
+CALLS = ((0, 2), (2, 6), (6, 7), (7, 8))
 GROUPS = ((0, 2), (2, 4), (4, 6), (6, 7), (7, 8))
 
 
@@ -33,8 +34,8 @@ def tile_moe_pln_glu_sigmoid_kernel(
     with ExitStack() as ctx:
         keep = ctx.enter_context(tc.tile_pool(name="keep", bufs=1))
         work = ctx.enter_context(tc.tile_pool(name="work", bufs=3))
-        ring = ctx.enter_context(tc.tile_pool(name="ring", bufs=2))
         psum = ctx.enter_context(tc.psum_pool(name="psum", bufs=2))
+        psum3 = ctx.enter_context(tc.psum_pool(name="psum3", bufs=3))
 
         offs_sb = keep.tile([P, E * C // 16], U16, name="offs_sb")
         pos1_sb = keep.tile([P, T // 16], U16, name="pos1_sb")
@@ -83,9 +84,9 @@ def tile_moe_pln_glu_sigmoid_kernel(
         load_words("w3", w3_words, 0, 2)
         load_scales(planes["w3"], w3_scales)
         load_words("w1", w1_words, 2, 5)
-        load_words("w3", w3_words, 2, 5)
+        load_words("w3", w3_words, 2, 4)
         load_words("w1", w1_words, 5, 8)
-        load_words("w3", w3_words, 5, 8)
+        load_words("w3", w3_words, 4, 8)
         load_scales(planes["w2"], w2_scales)
         load_words("w2", w2_words, 0, 8)
         nc.sync.dma_start(pos1_sb[:], pos1)
@@ -122,8 +123,8 @@ def tile_moe_pln_glu_sigmoid_kernel(
         live = {}
 
         def first_layer(e):
-            a_ps = psum.tile([C, H], F32, name="a_ps")
-            g_ps = psum.tile([C, H], F32, name="g_ps")
+            a_ps = psum3.tile([C, H], F32, name="a_ps")
+            g_ps = psum3.tile([C, H], F32, name="g_ps")
             for ps, label in ((a_ps, "w1"), (g_ps, "w3")):
                 nc.tensor.matmul_mx(
                     out=ps[:],
@@ -144,7 +145,7 @@ def tile_moe_pln_glu_sigmoid_kernel(
 
         def product(e):
             sig, g_ps = live[e]
-            h_row = work.tile([C, H], BF16, name="h_row", align_bytes=64)
+            h_row = keep.tile([C, H], BF16, name=f"h_row{e}", align_bytes=64)
             nc.vector.tensor_tensor(
                 h_row[:].rearrange("c (u m d) -> c u m d", u=2, d=2),
                 sig[:].rearrange("c (u m d) -> c u m d", u=2, d=2),
@@ -153,31 +154,37 @@ def tile_moe_pln_glu_sigmoid_kernel(
             )
             live[e] = h_row
 
+        h_grp = {
+            (lo, hi): keep.tile([P, (hi - lo) * C * 4], BF16, name=f"h_grp{lo}", align_bytes=64) for lo, hi in CALLS
+        }
+        call_of = {e: (lo, hi) for lo, hi in CALLS for e in range(lo, hi)}
+
         def turn_h(lo, hi):
             turn = psum.tile([P, hi - lo, 2, C], F32, name="turn")
             for e in range(lo, hi):
                 h_pairs = live[e][:].bitcast(F32)
                 for u in range(2):
                     nc.tensor.transpose(turn[:, e - lo, u, :], h_pairs[:, u * P : (u + 1) * P], ident[:])
-            h_grp = ring.tile([P, (hi - lo) * C * 4], BF16, name="h_grp", align_bytes=64)
+            first, last = call_of[lo]
             nc.scalar.copy(
-                out=h_grp[:].bitcast(F32).rearrange("p (e c u) -> p e c u", u=2, c=C),
+                out=h_grp[first, last][:, (lo - first) * C * 4 : (hi - first) * C * 4]
+                .bitcast(F32)
+                .rearrange("p (e c u) -> p e c u", u=2, c=C),
                 in_=turn[:].rearrange("p e u c -> p e c u"),
             )
-            live[lo, hi] = h_grp
 
         h_words, h_bytes = {}, {}
 
         def quantise_h(lo, hi):
             words = keep.tile([P, (hi - lo) * C], U32, name=f"h_words{lo}", align_bytes=64)
             scales = keep.tile([P, (hi - lo) * C], U8, name=f"h_bytes{lo}", align_bytes=64)
-            nc.vector.quantize_mx(out=words[:].bitcast(FP8X4), scales=scales[:], in_=live[lo, hi][:])
+            nc.vector.quantize_mx(out=words[:].bitcast(FP8X4), scales=scales[:], in_=h_grp[lo, hi][:])
             for e in range(lo, hi):
                 h_words[e] = words[:, (e - lo) * C : (e - lo + 1) * C]
                 h_bytes[e] = scales[:, (e - lo) * C : (e - lo + 1) * C]
 
         def second_layer(n, lo, hi, tag, copy):
-            y_ps = psum.tile([P, (hi - lo) * C], F32, name=tag)
+            y_ps = (psum if tag == "turn" else psum3).tile([P, (hi - lo) * C], F32, name=tag)
             for e in range(lo, hi):
                 nc.tensor.matmul_mx(
                     out=y_ps[:, (e - lo) * C : (e - lo + 1) * C],
@@ -190,28 +197,27 @@ def tile_moe_pln_glu_sigmoid_kernel(
                 )
             copy(out=y_sb[n][:, lo * C : hi * C], in_=y_ps[:])
 
-        ends_at = {hi - 1: (lo, hi) for lo, hi in GROUPS}
         gather(0, 2)
         gather(2, 1)
         first_layer(0)
         first_layer(1)
-        for s in range(E + 1):
-            if s < E:
-                product(s)
+        for s in range(E):
+            product(s)
             if s + 2 < E:
                 first_layer(s + 2)
-            if s - 1 in ends_at:
-                quantise_h(*ends_at[s - 1])
-            if s in ends_at:
-                turn_h(*ends_at[s])
+            for lo, hi in GROUPS:
+                if s == (hi - 1 if lo != 2 else E - 3):
+                    turn_h(lo, hi)
             if s % 2 == 1 and s + 3 < E:
                 gather(s + 3, 1)
-        second_layer(0, 0, QUAD, "y_ps", nc.scalar.copy)
-        second_layer(0, QUAD, E - 1, "y_ps", nc.vector.tensor_copy)
-        second_layer(0, E - 1, E, "turn", nc.vector.tensor_copy)
-        for n, tag in ((1, "a_ps"), (2, "g_ps")):
+        for lo, hi in CALLS:
+            quantise_h(lo, hi)
+        second_layer(0, 0, QUAD, "a_ps", nc.vector.tensor_copy)
+        second_layer(0, QUAD, E - 1, "a_ps", nc.scalar.copy)
+        second_layer(0, E - 1, E, "turn", nc.scalar.copy)
+        for n in range(1, NT):
             for lo in (0, QUAD):
-                second_layer(n, lo, lo + QUAD, tag, nc.scalar.copy)
+                second_layer(n, lo, lo + QUAD, "g_ps", nc.scalar.copy)
 
         parts = {}
 
@@ -242,7 +248,7 @@ def tile_moe_pln_glu_sigmoid_kernel(
                     )
             summed = work.tile([P, hi - lo], F32, name="summed")
             nc.scalar.copy(out=summed[:], in_=by_token[:])
-            by_row = psum.tile([P, hi - lo], F32, name="y_ps")
+            by_row = psum3.tile([P, hi - lo], F32, name="a_ps")
             for at in range(0, hi - lo, P):
                 nc.tensor.transpose(by_row[:, at : at + P], summed[:, at : at + P], ident[:])
             result = work.tile([P, hi - lo], F32, name="turned_back")

@@ -21,7 +21,7 @@ MULT = mybir.AluOpType.mult
 ADD = mybir.AluOpType.add
 SIGMOID = mybir.ActivationFunctionType.Sigmoid
 
-X_CHUNKS = ((0, 256), (256, 384), (384, 512))
+VECTOR_CAST = 320
 QUAD = 4
 CALLS = ((0, 2), (2, 6), (6, 7), (7, 8))
 GROUPS = ((0, 2), (2, 4), (4, 6), (6, 7), (7, 8))
@@ -41,13 +41,13 @@ def tile_moe_pln_glu_sigmoid_kernel(
         pos1_sb = keep.tile([P, T // 16], U16, name="pos1_sb")
         pos2_sb = keep.tile([P, T // 16], U16, name="pos2_sb")
 
-        x_raw = [keep.tile([P, 4, hi - lo], F32, name=f"x_raw{lo}") for lo, hi in X_CHUNKS]
-        x_grp = [keep.tile([P, hi - lo, 4], BF16, name=f"x_grp{lo}", align_bytes=64) for lo, hi in X_CHUNKS]
+        x_raw = [keep.tile([P, 2, T], F32, name=f"x_raw{i}") for i in range(2)]
+        x_grp = [keep.tile([P, HALF, 4], BF16, name=f"x_grp{i}", align_bytes=64) for i in range(2)]
         x_words = keep.tile([P, T], U32, name="x_words", align_bytes=64)
         x_bytes = keep.tile([P, T], U8, name="x_bytes", align_bytes=64)
         xv = xT.rearrange("(p j) t -> p j t", j=4)
-        for i, (lo, hi) in enumerate(X_CHUNKS):
-            nc.sync.dma_start(out=x_raw[i][:], in_=xv[:, :, lo:hi])
+        for i in range(2):
+            nc.sync.dma_start(out=x_raw[i][:], in_=xv[:, 2 * i : 2 * i + 2, :])
         nc.sync.dma_start(offs_sb[:], offs)
 
         def load_scales(plane, src):
@@ -79,8 +79,8 @@ def tile_moe_pln_glu_sigmoid_kernel(
             for e in range(lo, hi):
                 words_of[label, e] = tile[:, (e - lo) * width : (e - lo + 1) * width]
 
-        load_scales(planes["w1"], w1_scales)
         load_words("w1", w1_words, 0, 2)
+        load_scales(planes["w1"], w1_scales)
         load_words("w3", w3_words, 0, 2)
         load_scales(planes["w3"], w3_scales)
         load_words("w1", w1_words, 2, 5)
@@ -94,14 +94,16 @@ def tile_moe_pln_glu_sigmoid_kernel(
         gates = keep.tile([P, 2, T], F32, name="gates")
         nc.sync.dma_start(out=gates[:], in_=gate[:, :P, :].rearrange("g p t -> p g t"))
 
-        for i, (lo, hi) in enumerate(X_CHUNKS):
+        for i in range(2):
             src = x_raw[i][:].rearrange("p j t -> p t j")
-            split = (hi - lo) // 2
-            nc.vector.tensor_copy(out=x_grp[i][:, :split, :], in_=src[:, :split, :])
-            nc.scalar.copy(out=x_grp[i][:, split:, :], in_=src[:, split:, :])
+            pair = slice(2 * i, 2 * i + 2)
+            nc.vector.tensor_copy(out=x_grp[0][:, :, pair], in_=src[:, :HALF, :])
+            nc.vector.tensor_copy(out=x_grp[1][:, : VECTOR_CAST - HALF, pair], in_=src[:, HALF:VECTOR_CAST, :])
+            nc.scalar.copy(out=x_grp[1][:, VECTOR_CAST - HALF :, pair], in_=src[:, VECTOR_CAST:, :])
+        for i in range(2):
             nc.vector.quantize_mx(
-                out=x_words[:, lo:hi].bitcast(FP8X4),
-                scales=x_bytes[:, lo:hi],
+                out=x_words[:, i * HALF : (i + 1) * HALF].bitcast(FP8X4),
+                scales=x_bytes[:, i * HALF : (i + 1) * HALF],
                 in_=x_grp[i][:].rearrange("p t j -> p (t j)"),
             )
 

@@ -23,8 +23,9 @@ SIGMOID = mybir.ActivationFunctionType.Sigmoid
 
 VECTOR_CAST = 320
 QUAD = 4
-CALLS = ((0, 2), (2, 6), (6, 7), (7, 8))
-GROUPS = ((0, 2), (2, 4), (4, 6), (6, 7), (7, 8))
+CALLS = ((0, 4), (4, 6), (6, 8))
+ON_GPSIMD = (0, 1)
+A_BANKS = (0, 1, 2, 7)
 
 
 def tile_moe_pln_glu_sigmoid_kernel(
@@ -34,8 +35,8 @@ def tile_moe_pln_glu_sigmoid_kernel(
     with ExitStack() as ctx:
         keep = ctx.enter_context(tc.tile_pool(name="keep", bufs=1))
         work = ctx.enter_context(tc.tile_pool(name="work", bufs=3))
-        psum = ctx.enter_context(tc.psum_pool(name="psum", bufs=2))
-        psum3 = ctx.enter_context(tc.psum_pool(name="psum3", bufs=3))
+        psum = ctx.enter_context(tc.psum_pool(name="psum", bufs=1))
+        bank = [psum.tile([P, 512], F32, name=f"bank{i}") for i in range(8)]
 
         offs_sb = keep.tile([P, E * C // 16], U16, name="offs_sb")
         pos1_sb = keep.tile([P, T // 16], U16, name="pos1_sb")
@@ -83,9 +84,9 @@ def tile_moe_pln_glu_sigmoid_kernel(
         load_scales(planes["w1"], w1_scales)
         load_words("w3", w3_words, 0, 2)
         load_scales(planes["w3"], w3_scales)
-        load_words("w1", w1_words, 2, 5)
+        load_words("w1", w1_words, 2, 4)
         load_words("w3", w3_words, 2, 4)
-        load_words("w1", w1_words, 5, 8)
+        load_words("w1", w1_words, 4, 8)
         load_words("w3", w3_words, 4, 8)
         load_scales(planes["w2"], w2_scales)
         load_words("w2", w2_words, 0, 8)
@@ -110,8 +111,8 @@ def tile_moe_pln_glu_sigmoid_kernel(
         tok_words, tok_bytes = {}, {}
 
         def gather(lo, cuts):
-            gw = work.tile([P, 2 * C], U32, name="gw", align_bytes=64)
-            gb = work.tile([P, 2 * C], U8, name="gb", align_bytes=64)
+            gw = keep.tile([P, 2 * C], U32, name=f"gw{lo}", align_bytes=64)
+            gb = keep.tile([P, 2 * C], U8, name=f"gb{lo}", align_bytes=64)
             width = 2 * C // cuts
             for at in range(0, 2 * C, width):
                 part = offs_sb[:, (lo * C + at) // 16 : (lo * C + at + width) // 16]
@@ -124,30 +125,48 @@ def tile_moe_pln_glu_sigmoid_kernel(
         y_sb = [keep.tile([P, E * C], F32, name=f"y_sb{n}") for n in range(NT)]
         live = {}
 
-        def first_layer(e):
-            a_ps = psum3.tile([C, H], F32, name="a_ps")
-            g_ps = psum3.tile([C, H], F32, name="g_ps")
-            for ps, label in ((a_ps, "w1"), (g_ps, "w3")):
-                nc.tensor.matmul_mx(
-                    out=ps[:],
-                    lhsT=tok_words[e].bitcast(FP8X4),
-                    lhsT_scale=tok_bytes[e],
-                    rhs=words_of[label, e].bitcast(FP4X4),
-                    rhs_scale=planes[label][:, e * H : (e + 1) * H],
-                    start=True,
-                    stop=True,
-                )
-            sig = keep.tile([C, H], F32, name=f"sig{e}")
+        sigs = {}
+
+        def first_pass(ps, label, e):
+            nc.tensor.matmul_mx(
+                out=ps[:],
+                lhsT=tok_words[e].bitcast(FP8X4),
+                lhsT_scale=tok_bytes[e],
+                rhs=words_of[label, e].bitcast(FP4X4),
+                rhs_scale=planes[label][:, e * H : (e + 1) * H],
+                start=True,
+                stop=True,
+            )
+
+        def sigmoid_of(e):
+            a_ps = bank[A_BANKS[e % 4]]
+            first_pass(a_ps, "w1", e)
+            sigs[e] = keep.tile([C, H], F32, name=f"sig{e}")
             nc.scalar.activation(
-                sig[:].rearrange("c (u m d) -> c u m d", u=2, d=2),
+                sigs[e][:].rearrange("c (u m d) -> c u m d", u=2, d=2),
                 a_ps[:].rearrange("c (m u d) -> c u m d", u=2, d=2),
                 SIGMOID,
             )
-            live[e] = (sig, g_ps)
+
+        def linear_of(e):
+            g_ps = bank[3 + e % 4]
+            first_pass(g_ps, "w3", e)
+            live[e] = g_ps
+            if e in ON_GPSIMD:
+                g_sb = keep.tile([C, H], F32, name=f"g_sb{e}")
+                nc.scalar.copy(
+                    out=g_sb[:].rearrange("c (u m d) -> c u m d", u=2, d=2),
+                    in_=g_ps[:].rearrange("c (m u d) -> c u m d", u=2, d=2),
+                )
+                live[e] = g_sb
 
         def product(e):
-            sig, g_ps = live[e]
+            sig, g_ps = sigs[e], live[e]
             h_row = keep.tile([C, H], BF16, name=f"h_row{e}", align_bytes=64)
+            if e in ON_GPSIMD:
+                nc.gpsimd.tensor_tensor(h_row[:], sig[:], g_ps[:], MULT)
+                live[e] = h_row
+                return
             nc.vector.tensor_tensor(
                 h_row[:].rearrange("c (u m d) -> c u m d", u=2, d=2),
                 sig[:].rearrange("c (u m d) -> c u m d", u=2, d=2),
@@ -161,8 +180,8 @@ def tile_moe_pln_glu_sigmoid_kernel(
         }
         call_of = {e: (lo, hi) for lo, hi in CALLS for e in range(lo, hi)}
 
-        def turn_h(lo, hi):
-            turn = psum.tile([P, hi - lo, 2, C], F32, name="turn")
+        def turn_h(lo, hi, ps):
+            turn = ps[:, : (hi - lo) * 2 * C].rearrange("p (e u c) -> p e u c", u=2, c=C)
             for e in range(lo, hi):
                 h_pairs = live[e][:].bitcast(F32)
                 for u in range(2):
@@ -172,7 +191,7 @@ def tile_moe_pln_glu_sigmoid_kernel(
                 out=h_grp[first, last][:, (lo - first) * C * 4 : (hi - first) * C * 4]
                 .bitcast(F32)
                 .rearrange("p (e c u) -> p e c u", u=2, c=C),
-                in_=turn[:].rearrange("p e u c -> p e c u"),
+                in_=turn.rearrange("p e u c -> p e c u"),
             )
 
         h_words, h_bytes = {}, {}
@@ -185,8 +204,8 @@ def tile_moe_pln_glu_sigmoid_kernel(
                 h_words[e] = words[:, (e - lo) * C : (e - lo + 1) * C]
                 h_bytes[e] = scales[:, (e - lo) * C : (e - lo + 1) * C]
 
-        def second_layer(n, lo, hi, tag, copy):
-            y_ps = (psum if tag == "turn" else psum3).tile([P, (hi - lo) * C], F32, name=tag)
+        def second_layer(n, lo, hi, ps, copy):
+            y_ps = ps[:, : (hi - lo) * C]
             for e in range(lo, hi):
                 nc.tensor.matmul_mx(
                     out=y_ps[:, (e - lo) * C : (e - lo + 1) * C],
@@ -197,29 +216,36 @@ def tile_moe_pln_glu_sigmoid_kernel(
                     start=True,
                     stop=True,
                 )
-            copy(out=y_sb[n][:, lo * C : hi * C], in_=y_ps[:])
+            copy(out=y_sb[n][:, lo * C : hi * C], in_=y_ps)
 
         gather(0, 2)
-        gather(2, 1)
-        first_layer(0)
-        first_layer(1)
-        for s in range(E):
-            product(s)
-            if s + 2 < E:
-                first_layer(s + 2)
-            for lo, hi in GROUPS:
-                if s == (hi - 1 if lo != 2 else E - 3):
-                    turn_h(lo, hi)
-            if s % 2 == 1 and s + 3 < E:
-                gather(s + 3, 1)
+        for lo in range(2, E, 2):
+            gather(lo, 1)
+        for lo in (0, 2):
+            for e in (lo, lo + 1):
+                sigmoid_of(e)
+            for e in (lo, lo + 1):
+                linear_of(e)
+        for e in range(QUAD, E):
+            sigmoid_of(e)
+        for e in range(E):
+            product(e)
+            if e + QUAD < E:
+                linear_of(e + QUAD)
+        turn_h(0, 2, bank[3])
+        turn_h(2, 4, bank[4])
+        turn_h(4, 6, bank[0])
+        turn_h(6, 7, bank[1])
+        turn_h(7, 8, bank[2])
         for lo, hi in CALLS:
             quantise_h(lo, hi)
-        second_layer(0, 0, QUAD, "a_ps", nc.vector.tensor_copy)
-        second_layer(0, QUAD, E - 1, "a_ps", nc.scalar.copy)
-        second_layer(0, E - 1, E, "turn", nc.scalar.copy)
-        for n in range(1, NT):
-            for lo in (0, QUAD):
-                second_layer(n, lo, lo + QUAD, "g_ps", nc.scalar.copy)
+        second_layer(0, 0, QUAD, bank[7], nc.vector.tensor_copy)
+        second_layer(0, QUAD, 6, bank[5], nc.scalar.copy)
+        second_layer(0, 6, E, bank[6], nc.scalar.copy)
+        second_layer(1, 0, QUAD, bank[3], nc.scalar.copy)
+        second_layer(1, QUAD, E, bank[4], nc.scalar.copy)
+        second_layer(2, 0, QUAD, bank[0], nc.scalar.copy)
+        second_layer(2, QUAD, E, bank[1], nc.scalar.copy)
 
         parts = {}
 
@@ -237,7 +263,7 @@ def tile_moe_pln_glu_sigmoid_kernel(
             nc.sync.dma_start(out=out[n * P : (n + 1) * P, lo:hi], in_=result[:])
 
         def add_on_tensor(n, lo, hi):
-            by_token = psum.tile([P, hi - lo], F32, name="turn")
+            by_token = bank[(2, 5)[lo // HALF]][:, : hi - lo]
             for at in range(0, hi - lo, P):
                 for which in range(2):
                     nc.tensor.matmul(
@@ -249,12 +275,12 @@ def tile_moe_pln_glu_sigmoid_kernel(
                         stop=which == 1,
                     )
             summed = work.tile([P, hi - lo], F32, name="summed")
-            nc.scalar.copy(out=summed[:], in_=by_token[:])
-            by_row = psum3.tile([P, hi - lo], F32, name="a_ps")
+            nc.scalar.copy(out=summed[:], in_=by_token)
+            by_row = bank[(7, 6)[lo // HALF]][:, : hi - lo]
             for at in range(0, hi - lo, P):
                 nc.tensor.transpose(by_row[:, at : at + P], summed[:, at : at + P], ident[:])
             result = work.tile([P, hi - lo], F32, name="turned_back")
-            nc.scalar.copy(out=result[:], in_=by_row[:])
+            nc.scalar.copy(out=result[:], in_=by_row)
             nc.sync.dma_start(out=out[n * P : (n + 1) * P, lo:hi], in_=result[:])
 
         for n in range(NT - 1):

@@ -23,8 +23,8 @@ SIGMOID = mybir.ActivationFunctionType.Sigmoid
 
 VECTOR_CAST = 320
 QUAD = 4
-CALLS = ((0, 4), (4, 6), (6, 8))
-ON_GPSIMD = (0, 1)
+CALLS = ((0, 4), (4, 6), (6, 7), (7, 8))
+ON_GPSIMD = ()
 A_BANKS = (0, 1, 2, 7)
 
 
@@ -232,20 +232,20 @@ def tile_moe_pln_glu_sigmoid_kernel(
             product(e)
             if e + QUAD < E:
                 linear_of(e + QUAD)
-        turn_h(0, 2, bank[3])
-        turn_h(2, 4, bank[4])
+        turn_h(0, 2, bank[1])
+        turn_h(2, 4, bank[2])
         turn_h(4, 6, bank[0])
-        turn_h(6, 7, bank[1])
-        turn_h(7, 8, bank[2])
+        turn_h(6, 7, bank[3])
+        turn_h(7, 8, bank[4])
         for lo, hi in CALLS:
             quantise_h(lo, hi)
         second_layer(0, 0, QUAD, bank[7], nc.vector.tensor_copy)
-        second_layer(0, QUAD, 6, bank[5], nc.scalar.copy)
-        second_layer(0, 6, E, bank[6], nc.scalar.copy)
-        second_layer(1, 0, QUAD, bank[3], nc.scalar.copy)
-        second_layer(1, QUAD, E, bank[4], nc.scalar.copy)
+        second_layer(0, QUAD, E - 1, bank[5], nc.scalar.copy)
+        second_layer(0, E - 1, E, bank[6], nc.scalar.copy)
+        second_layer(1, 0, QUAD, bank[1], nc.scalar.copy)
+        second_layer(1, QUAD, E, bank[2], nc.scalar.copy)
         second_layer(2, 0, QUAD, bank[0], nc.scalar.copy)
-        second_layer(2, QUAD, E, bank[1], nc.scalar.copy)
+        second_layer(2, QUAD, E, bank[3], nc.scalar.copy)
 
         parts = {}
 
@@ -263,7 +263,7 @@ def tile_moe_pln_glu_sigmoid_kernel(
             nc.sync.dma_start(out=out[n * P : (n + 1) * P, lo:hi], in_=result[:])
 
         def add_on_tensor(n, lo, hi):
-            by_token = bank[(2, 5)[lo // HALF]][:, : hi - lo]
+            by_token = bank[(4, 5)[lo // HALF]][:, : hi - lo]
             for at in range(0, hi - lo, P):
                 for which in range(2):
                     nc.tensor.matmul(

@@ -23,7 +23,7 @@ SIGMOID = mybir.ActivationFunctionType.Sigmoid
 
 VECTOR_CAST = 320
 QUAD = 4
-CALLS = ((0, 4), (4, 6), (6, 7), (7, 8))
+CALLS = ((0, 2), (2, 4), (4, 6), (6, 7), (7, 8))
 ON_GPSIMD = ()
 A_BANKS = (0, 1, 2, 7)
 
@@ -87,13 +87,29 @@ def tile_moe_pln_glu_sigmoid_kernel(
         load_words("w1", w1_words, 2, 4)
         load_words("w3", w3_words, 2, 4)
         load_words("w1", w1_words, 4, 8)
-        load_words("w3", w3_words, 4, 8)
+        load_words("w3", w3_words, 4, 6)
+        load_words("w3", w3_words, 6, 8)
         load_scales(planes["w2"], w2_scales)
-        load_words("w2", w2_words, 0, 8)
+        w2_of = {}
+
+        def load_w2(first, last):
+            width = 2 * P * (last - first)
+            tile = keep.tile([P, E * width], U8, name=f"w2_{first}", align_bytes=64)
+            nc.sync.dma_start(
+                out=tile[:].bitcast(I32).rearrange("p (e n) -> p e n", e=E),
+                in_=w2_words[:, 0, :, 2 * P * first : 2 * P * last].rearrange("e p n -> p e n").bitcast(I32),
+            )
+            for e in range(E):
+                for n in range(first, last):
+                    at = e * width + 2 * P * (n - first)
+                    w2_of[e, n] = tile[:, at : at + 2 * P]
+
+        load_w2(0, 1)
         nc.sync.dma_start(pos1_sb[:], pos1)
         nc.sync.dma_start(pos2_sb[:], pos2)
         gates = keep.tile([P, 2, T], F32, name="gates")
         nc.sync.dma_start(out=gates[:], in_=gate[:, :P, :].rearrange("g p t -> p g t"))
+        load_w2(1, NT)
 
         for i in range(2):
             src = x_raw[i][:].rearrange("p j t -> p t j")
@@ -209,7 +225,7 @@ def tile_moe_pln_glu_sigmoid_kernel(
             for e in range(lo, hi):
                 nc.tensor.matmul_mx(
                     out=y_ps[:, (e - lo) * C : (e - lo + 1) * C],
-                    lhsT=words_of["w2", e][:, 2 * P * n : 2 * P * (n + 1)].bitcast(FP4X4),
+                    lhsT=w2_of[e, n].bitcast(FP4X4),
                     lhsT_scale=planes["w2"][:, e * N + n * P : e * N + (n + 1) * P],
                     rhs=h_words[e].bitcast(FP8X4),
                     rhs_scale=h_bytes[e],
@@ -240,8 +256,8 @@ def tile_moe_pln_glu_sigmoid_kernel(
         for lo, hi in CALLS:
             quantise_h(lo, hi)
         second_layer(0, 0, QUAD, bank[7], nc.vector.tensor_copy)
-        second_layer(0, QUAD, E - 1, bank[5], nc.scalar.copy)
-        second_layer(0, E - 1, E, bank[6], nc.scalar.copy)
+        second_layer(0, QUAD, 6, bank[5], nc.scalar.copy)
+        second_layer(0, 6, E, bank[6], nc.scalar.copy)
         second_layer(1, 0, QUAD, bank[1], nc.scalar.copy)
         second_layer(1, QUAD, E, bank[2], nc.scalar.copy)
         second_layer(2, 0, QUAD, bank[0], nc.scalar.copy)
@@ -263,7 +279,7 @@ def tile_moe_pln_glu_sigmoid_kernel(
             nc.sync.dma_start(out=out[n * P : (n + 1) * P, lo:hi], in_=result[:])
 
         def add_on_tensor(n, lo, hi):
-            by_token = bank[(4, 5)[lo // HALF]][:, : hi - lo]
+            by_token = bank[(0, 3)[lo // HALF]][:, : hi - lo]
             for at in range(0, hi - lo, P):
                 for which in range(2):
                     nc.tensor.matmul(
@@ -281,7 +297,7 @@ def tile_moe_pln_glu_sigmoid_kernel(
                 nc.tensor.transpose(by_row[:, at : at + P], summed[:, at : at + P], ident[:])
             result = work.tile([P, hi - lo], F32, name="turned_back")
             nc.scalar.copy(out=result[:], in_=by_row)
-            nc.sync.dma_start(out=out[n * P : (n + 1) * P, lo:hi], in_=result[:])
+            nc.scalar.dma_start(out=out[n * P : (n + 1) * P, lo:hi], in_=result[:])
 
         for n in range(NT - 1):
             for lo in (0, HALF):

@@ -24,8 +24,8 @@ SIGMOID = mybir.ActivationFunctionType.Sigmoid
 VECTOR_CAST = 320
 QUAD = 4
 CALLS = ((0, 2), (2, 4), (4, 6), (6, 7), (7, 8))
-ON_GPSIMD = ()
-A_BANKS = (0, 1, 2, 7)
+A_BANKS = (0, 1, 2, 3, 0, 1, 2, 3)
+G_BANKS = (4, 5, 6, 7, 0, 1, 4, 5)
 
 
 def tile_moe_pln_glu_sigmoid_kernel(
@@ -82,11 +82,12 @@ def tile_moe_pln_glu_sigmoid_kernel(
 
         load_words("w1", w1_words, 0, 2)
         load_scales(planes["w1"], w1_scales)
-        load_words("w3", w3_words, 0, 2)
         load_scales(planes["w3"], w3_scales)
+        load_words("w3", w3_words, 0, 2)
         load_words("w1", w1_words, 2, 4)
+        load_words("w1", w1_words, 4, 6)
+        load_words("w1", w1_words, 6, 8)
         load_words("w3", w3_words, 2, 4)
-        load_words("w1", w1_words, 4, 8)
         load_words("w3", w3_words, 4, 6)
         load_words("w3", w3_words, 6, 8)
         load_scales(planes["w2"], w2_scales)
@@ -155,7 +156,7 @@ def tile_moe_pln_glu_sigmoid_kernel(
             )
 
         def sigmoid_of(e):
-            a_ps = bank[A_BANKS[e % 4]]
+            a_ps = bank[A_BANKS[e]]
             first_pass(a_ps, "w1", e)
             sigs[e] = keep.tile([C, H], F32, name=f"sig{e}")
             nc.scalar.activation(
@@ -165,24 +166,13 @@ def tile_moe_pln_glu_sigmoid_kernel(
             )
 
         def linear_of(e):
-            g_ps = bank[3 + e % 4]
+            g_ps = bank[G_BANKS[e]]
             first_pass(g_ps, "w3", e)
             live[e] = g_ps
-            if e in ON_GPSIMD:
-                g_sb = keep.tile([C, H], F32, name=f"g_sb{e}")
-                nc.scalar.copy(
-                    out=g_sb[:].rearrange("c (u m d) -> c u m d", u=2, d=2),
-                    in_=g_ps[:].rearrange("c (m u d) -> c u m d", u=2, d=2),
-                )
-                live[e] = g_sb
 
         def product(e):
             sig, g_ps = sigs[e], live[e]
             h_row = keep.tile([C, H], BF16, name=f"h_row{e}", align_bytes=64)
-            if e in ON_GPSIMD:
-                nc.gpsimd.tensor_tensor(h_row[:], sig[:], g_ps[:], MULT)
-                live[e] = h_row
-                return
             nc.vector.tensor_tensor(
                 h_row[:].rearrange("c (u m d) -> c u m d", u=2, d=2),
                 sig[:].rearrange("c (u m d) -> c u m d", u=2, d=2),
@@ -237,31 +227,32 @@ def tile_moe_pln_glu_sigmoid_kernel(
         gather(0, 2)
         for lo in range(2, E, 2):
             gather(lo, 1)
-        for lo in (0, 2):
-            for e in (lo, lo + 1):
-                sigmoid_of(e)
-            for e in (lo, lo + 1):
-                linear_of(e)
-        for e in range(QUAD, E):
+        for e in range(2):
             sigmoid_of(e)
+        for e in range(2):
+            linear_of(e)
+        for e in range(2, E):
+            sigmoid_of(e)
+        for e in range(2, 6):
+            linear_of(e)
         for e in range(E):
             product(e)
-            if e + QUAD < E:
-                linear_of(e + QUAD)
-        turn_h(0, 2, bank[1])
+            if e < 2:
+                linear_of(e + 6)
+        turn_h(0, 2, bank[3])
         turn_h(2, 4, bank[2])
-        turn_h(4, 6, bank[0])
-        turn_h(6, 7, bank[3])
-        turn_h(7, 8, bank[4])
+        turn_h(4, 6, bank[6])
+        turn_h(6, 7, bank[7])
+        turn_h(7, 8, bank[0])
         for lo, hi in CALLS:
             quantise_h(lo, hi)
-        second_layer(0, 0, QUAD, bank[7], nc.vector.tensor_copy)
-        second_layer(0, QUAD, 6, bank[5], nc.scalar.copy)
-        second_layer(0, 6, E, bank[6], nc.scalar.copy)
-        second_layer(1, 0, QUAD, bank[1], nc.scalar.copy)
-        second_layer(1, QUAD, E, bank[2], nc.scalar.copy)
-        second_layer(2, 0, QUAD, bank[0], nc.scalar.copy)
-        second_layer(2, QUAD, E, bank[3], nc.scalar.copy)
+        second_layer(0, 0, QUAD, bank[1], nc.vector.tensor_copy)
+        second_layer(0, QUAD, 7, bank[3], nc.scalar.copy)
+        second_layer(0, 7, E, bank[4], nc.scalar.copy)
+        second_layer(1, 0, QUAD, bank[5], nc.scalar.copy)
+        second_layer(1, QUAD, E, bank[6], nc.scalar.copy)
+        second_layer(2, 0, QUAD, bank[7], nc.scalar.copy)
+        second_layer(2, QUAD, E, bank[0], nc.scalar.copy)
 
         parts = {}
 
@@ -279,7 +270,7 @@ def tile_moe_pln_glu_sigmoid_kernel(
             nc.sync.dma_start(out=out[n * P : (n + 1) * P, lo:hi], in_=result[:])
 
         def add_on_tensor(n, lo, hi):
-            by_token = bank[(0, 3)[lo // HALF]][:, : hi - lo]
+            by_token = bank[(7, 0)[lo // HALF]][:, : hi - lo]
             for at in range(0, hi - lo, P):
                 for which in range(2):
                     nc.tensor.matmul(
@@ -292,7 +283,7 @@ def tile_moe_pln_glu_sigmoid_kernel(
                     )
             summed = work.tile([P, hi - lo], F32, name="summed")
             nc.scalar.copy(out=summed[:], in_=by_token)
-            by_row = bank[(7, 6)[lo // HALF]][:, : hi - lo]
+            by_row = bank[(2, 3)[lo // HALF]][:, : hi - lo]
             for at in range(0, hi - lo, P):
                 nc.tensor.transpose(by_row[:, at : at + P], summed[:, at : at + P], ident[:])
             result = work.tile([P, hi - lo], F32, name="turned_back")

@@ -23,9 +23,10 @@ SIGMOID = mybir.ActivationFunctionType.Sigmoid
 
 VECTOR_CAST = 320
 QUAD = 4
-CALLS = ((0, 2), (2, 4), (4, 6), (6, 7), (7, 8))
+GROUPS = ((1, 2), (3, 4), (5, 0), (6,), (7,))
 A_BANKS = (0, 1, 2, 3, 0, 1, 2, 3)
 G_BANKS = (4, 5, 6, 7, 0, 1, 4, 5)
+ON_GPSIMD = (0,)
 
 
 def tile_moe_pln_glu_sigmoid_kernel(
@@ -45,7 +46,7 @@ def tile_moe_pln_glu_sigmoid_kernel(
         x_raw = [keep.tile([P, 2, T], F32, name=f"x_raw{i}") for i in range(2)]
         x_grp = [keep.tile([P, HALF, 4], BF16, name=f"x_grp{i}", align_bytes=64) for i in range(2)]
         x_words = keep.tile([P, T], U32, name="x_words", align_bytes=64)
-        x_bytes = keep.tile([P, T], U8, name="x_bytes", align_bytes=64)
+        x_bytes = keep.tile([P, T], U8, name="x_bytes", tag="x_bytes", align_bytes=64)
         xv = xT.rearrange("(p j) t -> p j t", j=4)
         for i in range(2):
             nc.sync.dma_start(out=x_raw[i][:], in_=xv[:, 2 * i : 2 * i + 2, :])
@@ -86,8 +87,8 @@ def tile_moe_pln_glu_sigmoid_kernel(
         load_words("w3", w3_words, 0, 2)
         load_words("w1", w1_words, 2, 4)
         load_words("w1", w1_words, 4, 6)
-        load_words("w1", w1_words, 6, 8)
         load_words("w3", w3_words, 2, 4)
+        load_words("w1", w1_words, 6, 8)
         load_words("w3", w3_words, 4, 6)
         load_words("w3", w3_words, 6, 8)
         load_scales(planes["w2"], w2_scales)
@@ -169,9 +170,22 @@ def tile_moe_pln_glu_sigmoid_kernel(
             g_ps = bank[G_BANKS[e]]
             first_pass(g_ps, "w3", e)
             live[e] = g_ps
+            if e in ON_GPSIMD:
+                g_sb = keep.tile([C, H], F32, name=f"g_sb{e}")
+                nc.scalar.copy(
+                    out=g_sb[:].rearrange("c (u m d) -> c u m d", u=2, d=2),
+                    in_=g_ps[:].rearrange("c (m u d) -> c u m d", u=2, d=2),
+                )
+                live[e] = g_sb
 
         def product(e):
             sig, g_ps = sigs[e], live[e]
+            if e in ON_GPSIMD:
+                held = "x_bytes" if e == ON_GPSIMD[0] else f"h_row{e}"
+                h_row = keep.tile([C, H], BF16, name=f"h_row{e}", tag=held, align_bytes=64)
+                nc.gpsimd.tensor_tensor(h_row[:], sig[:], g_ps[:], MULT)
+                live[e] = h_row
+                return
             h_row = keep.tile([C, H], BF16, name=f"h_row{e}", align_bytes=64)
             nc.vector.tensor_tensor(
                 h_row[:].rearrange("c (u m d) -> c u m d", u=2, d=2),
@@ -182,33 +196,29 @@ def tile_moe_pln_glu_sigmoid_kernel(
             live[e] = h_row
 
         h_grp = {
-            (lo, hi): keep.tile([P, (hi - lo) * C * 4], BF16, name=f"h_grp{lo}", align_bytes=64) for lo, hi in CALLS
+            group: keep.tile([P, len(group) * C * 4], BF16, name=f"h_grp{group[0]}", align_bytes=64) for group in GROUPS
         }
-        call_of = {e: (lo, hi) for lo, hi in CALLS for e in range(lo, hi)}
 
-        def turn_h(lo, hi, ps):
-            turn = ps[:, : (hi - lo) * 2 * C].rearrange("p (e u c) -> p e u c", u=2, c=C)
-            for e in range(lo, hi):
+        def turn_h(group, ps):
+            turn = ps[:, : len(group) * 2 * C].rearrange("p (e u c) -> p e u c", u=2, c=C)
+            for at, e in enumerate(group):
                 h_pairs = live[e][:].bitcast(F32)
                 for u in range(2):
-                    nc.tensor.transpose(turn[:, e - lo, u, :], h_pairs[:, u * P : (u + 1) * P], ident[:])
-            first, last = call_of[lo]
+                    nc.tensor.transpose(turn[:, at, u, :], h_pairs[:, u * P : (u + 1) * P], ident[:])
             nc.scalar.copy(
-                out=h_grp[first, last][:, (lo - first) * C * 4 : (hi - first) * C * 4]
-                .bitcast(F32)
-                .rearrange("p (e c u) -> p e c u", u=2, c=C),
+                out=h_grp[group][:].bitcast(F32).rearrange("p (e c u) -> p e c u", u=2, c=C),
                 in_=turn.rearrange("p e u c -> p e c u"),
             )
 
         h_words, h_bytes = {}, {}
 
-        def quantise_h(lo, hi):
-            words = keep.tile([P, (hi - lo) * C], U32, name=f"h_words{lo}", align_bytes=64)
-            scales = keep.tile([P, (hi - lo) * C], U8, name=f"h_bytes{lo}", align_bytes=64)
-            nc.vector.quantize_mx(out=words[:].bitcast(FP8X4), scales=scales[:], in_=h_grp[lo, hi][:])
-            for e in range(lo, hi):
-                h_words[e] = words[:, (e - lo) * C : (e - lo + 1) * C]
-                h_bytes[e] = scales[:, (e - lo) * C : (e - lo + 1) * C]
+        def quantise_h(group):
+            words = keep.tile([P, len(group) * C], U32, name=f"h_words{group[0]}", align_bytes=64)
+            scales = keep.tile([P, len(group) * C], U8, name=f"h_bytes{group[0]}", align_bytes=64)
+            nc.vector.quantize_mx(out=words[:].bitcast(FP8X4), scales=scales[:], in_=h_grp[group][:])
+            for at, e in enumerate(group):
+                h_words[e] = words[:, at * C : (at + 1) * C]
+                h_bytes[e] = scales[:, at * C : (at + 1) * C]
 
         def second_layer(n, lo, hi, ps, copy):
             y_ps = ps[:, : (hi - lo) * C]
@@ -231,23 +241,25 @@ def tile_moe_pln_glu_sigmoid_kernel(
             sigmoid_of(e)
         for e in range(2):
             linear_of(e)
-        for e in range(2, E):
-            sigmoid_of(e)
         for e in range(2, 6):
+            sigmoid_of(e)
+        for e in range(2, 4):
+            linear_of(e)
+        for e in range(6, E):
+            sigmoid_of(e)
+        for e in range(4, 6):
             linear_of(e)
         for e in range(E):
             product(e)
             if e < 2:
                 linear_of(e + 6)
-        turn_h(0, 2, bank[3])
-        turn_h(2, 4, bank[2])
-        turn_h(4, 6, bank[6])
-        turn_h(6, 7, bank[7])
-        turn_h(7, 8, bank[0])
-        for lo, hi in CALLS:
-            quantise_h(lo, hi)
-        second_layer(0, 0, QUAD, bank[1], nc.vector.tensor_copy)
-        second_layer(0, QUAD, 7, bank[3], nc.scalar.copy)
+        for group, at in zip(GROUPS, (2, 3, 6, 7, 0)):
+            turn_h(group, bank[at])
+        for group in GROUPS:
+            quantise_h(group)
+        second_layer(0, 1, 5, bank[1], nc.vector.tensor_copy)
+        second_layer(0, 0, 1, bank[3], nc.scalar.copy)
+        second_layer(0, 5, 7, bank[2], nc.scalar.copy)
         second_layer(0, 7, E, bank[4], nc.scalar.copy)
         second_layer(1, 0, QUAD, bank[5], nc.scalar.copy)
         second_layer(1, QUAD, E, bank[6], nc.scalar.copy)

@@ -23,6 +23,7 @@ SIGMOID = mybir.ActivationFunctionType.Sigmoid
 
 VECTOR_CAST = 320
 QUAD = 4
+WARM_UP = 3
 GROUPS = ((1, 2), (3, 4), (5, 0), (6,), (7,))
 A_BANKS = (0, 1, 2, 3, 0, 1, 2, 3)
 G_BANKS = (4, 5, 6, 7, 0, 1, 4, 5)
@@ -69,6 +70,11 @@ def tile_moe_pln_glu_sigmoid_kernel(
         ident = keep.tile([P, P], F32, name="ident")
         make_identity(nc, ident[:])
 
+        slot_words = {lo: keep.tile([P, 2 * C], U32, name=f"gw{lo}", align_bytes=64) for lo in range(0, E, 2)}
+        slot_bytes = {lo: keep.tile([P, 2 * C], U8, name=f"gb{lo}", align_bytes=64) for lo in range(0, E, 2)}
+        nc.vector.memset(slot_words[E - 2][:, :C].bitcast(I32), 0)
+        nc.vector.memset(slot_bytes[E - 2][:, :C].bitcast(I32), 0)
+
         words_of = {}
 
         def load_words(label, words, lo, hi):
@@ -82,6 +88,16 @@ def tile_moe_pln_glu_sigmoid_kernel(
                 words_of[label, e] = tile[:, (e - lo) * width : (e - lo + 1) * width]
 
         load_words("w1", w1_words, 0, 2)
+        for i in range(WARM_UP):
+            nc.tensor.matmul_mx(
+                out=bank[7][:],
+                lhsT=slot_words[E - 2][:, :C].bitcast(FP8X4),
+                lhsT_scale=slot_bytes[E - 2][:, :C],
+                rhs=words_of["w1", 0].bitcast(FP4X4),
+                rhs_scale=planes["w2"][:, :H],
+                start=True,
+                stop=True,
+            )
         load_scales(planes["w1"], w1_scales)
         load_scales(planes["w3"], w3_scales)
         load_words("w3", w3_words, 0, 2)
@@ -129,8 +145,7 @@ def tile_moe_pln_glu_sigmoid_kernel(
         tok_words, tok_bytes = {}, {}
 
         def gather(lo, cuts):
-            gw = keep.tile([P, 2 * C], U32, name=f"gw{lo}", align_bytes=64)
-            gb = keep.tile([P, 2 * C], U8, name=f"gb{lo}", align_bytes=64)
+            gw, gb = slot_words[lo], slot_bytes[lo]
             width = 2 * C // cuts
             for at in range(0, 2 * C, width):
                 part = offs_sb[:, (lo * C + at) // 16 : (lo * C + at + width) // 16]

@@ -23,6 +23,7 @@ SIGMOID = mybir.ActivationFunctionType.Sigmoid
 
 VECTOR_CAST = 320
 QUAD = 4
+KEEP_WARM = 2
 WARM_UP = 3
 GROUPS = ((1, 2), (3, 4), (5, 0), (6,), (7,))
 A_BANKS = (0, 1, 2, 3, 0, 1, 2, 3)
@@ -268,7 +269,11 @@ def tile_moe_pln_glu_sigmoid_kernel(
             product(e)
             if e < 2:
                 linear_of(e + 6)
-        for group, at in zip(GROUPS, (2, 3, 6, 7, 0)):
+        for group, at in zip(GROUPS[:3], (2, 3, 6)):
+            turn_h(group, bank[at])
+        for i in range(KEEP_WARM):
+            first_pass(bank[1], "w3", E - 1)
+        for group, at in zip(GROUPS[3:], (7, 0)):
             turn_h(group, bank[at])
         for group in GROUPS:
             quantise_h(group)

@@ -24,7 +24,6 @@ SIGMOID = mybir.ActivationFunctionType.Sigmoid
 VECTOR_CAST = 320
 QUAD = 4
 KEEP_WARM = 2
-WARM_UP = 3
 GROUPS = ((1, 2), (3, 4), (5, 0), (6,), (7,))
 A_BANKS = (0, 1, 2, 3, 0, 1, 2, 3)
 G_BANKS = (4, 5, 6, 7, 0, 1, 4, 5)
@@ -73,8 +72,6 @@ def tile_moe_pln_glu_sigmoid_kernel(
 
         slot_words = {lo: keep.tile([P, 2 * C], U32, name=f"gw{lo}", align_bytes=64) for lo in range(0, E, 2)}
         slot_bytes = {lo: keep.tile([P, 2 * C], U8, name=f"gb{lo}", align_bytes=64) for lo in range(0, E, 2)}
-        nc.vector.memset(slot_words[E - 2][:, :C].bitcast(I32), 0)
-        nc.vector.memset(slot_bytes[E - 2][:, :C].bitcast(I32), 0)
 
         words_of = {}
 
@@ -89,16 +86,6 @@ def tile_moe_pln_glu_sigmoid_kernel(
                 words_of[label, e] = tile[:, (e - lo) * width : (e - lo + 1) * width]
 
         load_words("w1", w1_words, 0, 2)
-        for i in range(WARM_UP):
-            nc.tensor.matmul_mx(
-                out=bank[7][:],
-                lhsT=slot_words[E - 2][:, :C].bitcast(FP8X4),
-                lhsT_scale=slot_bytes[E - 2][:, :C],
-                rhs=words_of["w1", 0].bitcast(FP4X4),
-                rhs_scale=planes["w2"][:, :H],
-                start=True,
-                stop=True,
-            )
         load_scales(planes["w1"], w1_scales)
         load_scales(planes["w3"], w3_scales)
         load_words("w3", w3_words, 0, 2)

@@ -288,32 +288,43 @@ def tile_moe_pln_glu_sigmoid_kernel(
             nc.vector.tensor_tensor(result[:], parts[n, 0][:, lo:hi], parts[n, 1][:, lo:hi], ADD)
             nc.sync.dma_start(out=out[n * P : (n + 1) * P, lo:hi], in_=result[:])
 
-        def add_on_tensor(n, lo, hi):
-            by_token = bank[(7, 0)[lo // HALF]][:, : hi - lo]
+        def turn_part(n, which, lo, hi, ps):
             for at in range(0, hi - lo, P):
-                for which in range(2):
-                    nc.tensor.matmul(
-                        by_token[:, at : at + P],
-                        lhsT=parts[n, which][:, lo + at : lo + at + P],
-                        rhs=ident[:],
-                        is_transpose=True,
-                        start=which == 0,
-                        stop=which == 1,
-                    )
-            summed = work.tile([P, hi - lo], F32, name="summed")
-            nc.scalar.copy(out=summed[:], in_=by_token)
-            by_row = bank[(2, 3)[lo // HALF]][:, : hi - lo]
-            for at in range(0, hi - lo, P):
-                nc.tensor.transpose(by_row[:, at : at + P], summed[:, at : at + P], ident[:])
-            result = work.tile([P, hi - lo], F32, name="turned_back")
-            nc.scalar.copy(out=result[:], in_=by_row)
-            nc.scalar.dma_start(out=out[n * P : (n + 1) * P, lo:hi], in_=result[:])
+                nc.tensor.matmul(
+                    ps[:, at : at + P],
+                    lhsT=parts[n, which][:, lo + at : lo + at + P],
+                    rhs=ident[:],
+                    is_transpose=True,
+                    start=which == 0 and at == 0,
+                    stop=which == 1 and at + P == hi - lo,
+                )
 
-        for n in range(NT - 1):
-            for lo in (0, HALF):
-                pick(n, 0, lo, lo + HALF)
-                pick(n, 1, lo, lo + HALF)
-                add_on_tensor(n, lo, lo + HALF)
+        def turn_back(width, ps, by_row):
+            summed = work.tile([P, width], F32, name=f"summed{width}")
+            nc.scalar.copy(out=summed[:], in_=ps[:, :width])
+            for at in range(0, width, P):
+                nc.tensor.transpose(by_row[:, at : at + P], summed[:, at : at + P], ident[:])
+
+        def leave(n, lo, by_row):
+            result = work.tile([P, HALF], F32, name="turned_back")
+            nc.scalar.copy(out=result[:], in_=by_row[:, :HALF])
+            nc.scalar.dma_start(out=out[n * P : (n + 1) * P, lo : lo + HALF], in_=result[:])
+
+        for n, lo, ps, by_row in ((0, 0, bank[5], bank[2]), (0, HALF, bank[6], bank[3]), (1, 0, bank[5], bank[1])):
+            for which in range(2):
+                pick(n, which, lo, lo + HALF)
+            for which in range(2):
+                turn_part(n, which, lo, lo + HALF, ps)
+            turn_back(HALF, ps, by_row)
+            leave(n, lo, by_row)
+        last_blocks = ((HALF, bank[6]), (HALF + P, bank[2]))
+        for which in range(2):
+            pick(1, which, HALF, T)
+            for lo, ps in last_blocks:
+                turn_part(1, which, lo, lo + P, ps)
+        for lo, ps in last_blocks:
+            turn_back(P, ps, bank[3][:, lo - HALF : lo - HALF + P])
+        leave(1, HALF, bank[3])
         pick(NT - 1, 0, 0, T)
         pick(NT - 1, 1, 0, HALF)
         pick(NT - 1, 1, HALF, T)

@@ -20,14 +20,17 @@ FP4X4 = mybir.dt.float4_e2m1fn_x4
 MULT = mybir.AluOpType.mult
 ADD = mybir.AluOpType.add
 SIGMOID = mybir.ActivationFunctionType.Sigmoid
+COPY = mybir.ActivationFunctionType.Copy
 
 VECTOR_CAST = 320
 QUAD = 4
 KEEP_WARM = 2
-GROUPS = ((1, 2), (3, 4), (5, 0), (6,), (7,))
-A_BANKS = (0, 1, 2, 3, 0, 1, 2, 3)
-G_BANKS = (4, 5, 6, 7, 0, 1, 4, 5)
-ON_GPSIMD = (0,)
+ORDER = (5, 0, 1, 2, 3, 4, 6, 7)
+PAIRS = ((0, 5), (1, 2), (3, 4), (6, 7))
+GROUPS = ((0, 1), (2, 3), (4, 5), (6,), (7,))
+A_BANKS = dict(zip(ORDER, (0, 1, 2, 3, 0, 1, 2, 3)))
+G_BANKS = dict(zip(ORDER, (4, 5, 6, 7, 0, 1, 4, 5)))
+ON_GPSIMD = ORDER[:1]
 
 
 def tile_moe_pln_glu_sigmoid_kernel(
@@ -70,31 +73,32 @@ def tile_moe_pln_glu_sigmoid_kernel(
         ident = keep.tile([P, P], F32, name="ident")
         make_identity(nc, ident[:])
 
-        slot_words = {lo: keep.tile([P, 2 * C], U32, name=f"gw{lo}", align_bytes=64) for lo in range(0, E, 2)}
-        slot_bytes = {lo: keep.tile([P, 2 * C], U8, name=f"gb{lo}", align_bytes=64) for lo in range(0, E, 2)}
+        slot_words = {lo: keep.tile([P, 2 * C], U32, name=f"gw{lo}", align_bytes=64) for lo, hi in PAIRS}
+        slot_bytes = {lo: keep.tile([P, 2 * C], U8, name=f"gb{lo}", align_bytes=64) for lo, hi in PAIRS}
 
         words_of = {}
 
-        def load_words(label, words, lo, hi):
+        def load_words(label, words, pair):
+            lo, hi = pair
             width = words.shape[3]
-            tile = keep.tile([P, (hi - lo) * width], U8, name=f"{label}_{lo}", align_bytes=64)
+            tile = keep.tile([P, 2 * width], U8, name=f"{label}_{lo}", align_bytes=64)
             nc.sync.dma_start(
-                out=tile[:].bitcast(I32).rearrange("p (e n) -> p e n", e=hi - lo),
-                in_=words[lo:hi, 0].rearrange("e p n -> p e n").bitcast(I32),
+                out=tile[:].bitcast(I32).rearrange("p (e n) -> p e n", e=2),
+                in_=words[lo : hi + 1 : hi - lo, 0].rearrange("e p n -> p e n").bitcast(I32),
             )
-            for e in range(lo, hi):
-                words_of[label, e] = tile[:, (e - lo) * width : (e - lo + 1) * width]
+            for at, e in enumerate(pair):
+                words_of[label, e] = tile[:, at * width : (at + 1) * width]
 
-        load_words("w1", w1_words, 0, 2)
+        load_words("w1", w1_words, PAIRS[0])
         load_scales(planes["w1"], w1_scales)
         load_scales(planes["w3"], w3_scales)
-        load_words("w3", w3_words, 0, 2)
-        load_words("w1", w1_words, 2, 4)
-        load_words("w1", w1_words, 4, 6)
-        load_words("w3", w3_words, 2, 4)
-        load_words("w1", w1_words, 6, 8)
-        load_words("w3", w3_words, 4, 6)
-        load_words("w3", w3_words, 6, 8)
+        load_words("w3", w3_words, PAIRS[0])
+        load_words("w1", w1_words, PAIRS[1])
+        load_words("w1", w1_words, PAIRS[2])
+        load_words("w3", w3_words, PAIRS[1])
+        load_words("w1", w1_words, PAIRS[3])
+        load_words("w3", w3_words, PAIRS[2])
+        load_words("w3", w3_words, PAIRS[3])
         load_scales(planes["w2"], w2_scales)
         w2_of = {}
 
@@ -116,6 +120,9 @@ def tile_moe_pln_glu_sigmoid_kernel(
         gates = keep.tile([P, 2, T], F32, name="gates")
         nc.sync.dma_start(out=gates[:], in_=gate[:, :P, :].rearrange("g p t -> p g t"))
         load_w2(1, NT)
+        gate_col = keep.tile([P, T // P], F32, name="gate_col")
+        with nc.allow_non_contiguous_dma(reason="one gate value a partition"):
+            nc.sync.dma_start(out=gate_col[:], in_=gate[1, 0, :].rearrange("(b p) -> p b", p=P))
 
         for i in range(2):
             src = x_raw[i][:].rearrange("p j t -> p t j")
@@ -132,16 +139,16 @@ def tile_moe_pln_glu_sigmoid_kernel(
 
         tok_words, tok_bytes = {}, {}
 
-        def gather(lo, cuts):
-            gw, gb = slot_words[lo], slot_bytes[lo]
-            width = 2 * C // cuts
-            for at in range(0, 2 * C, width):
-                part = offs_sb[:, (lo * C + at) // 16 : (lo * C + at + width) // 16]
-                nc.vector.tensor_copy(gw[:, at : at + width], x_words[:].indirect(part))
-                nc.vector.tensor_copy(gb[:, at : at + width], x_bytes[:].indirect(part))
-            for e in range(lo, lo + 2):
-                tok_words[e] = gw[:, (e - lo) * C : (e - lo + 1) * C]
-                tok_bytes[e] = gb[:, (e - lo) * C : (e - lo + 1) * C]
+        def gather(pair, runs):
+            gw, gb = slot_words[pair[0]], slot_bytes[pair[0]]
+            for first_e, count in runs:
+                at = pair.index(first_e) * C
+                part = offs_sb[:, first_e * C // 16 : (first_e + count) * C // 16]
+                nc.vector.tensor_copy(gw[:, at : at + count * C], x_words[:].indirect(part))
+                nc.vector.tensor_copy(gb[:, at : at + count * C], x_bytes[:].indirect(part))
+            for at, e in enumerate(pair):
+                tok_words[e] = gw[:, at * C : (at + 1) * C]
+                tok_bytes[e] = gb[:, at * C : (at + 1) * C]
 
         y_sb = [keep.tile([P, E * C], F32, name=f"y_sb{n}") for n in range(NT)]
         live = {}
@@ -237,25 +244,25 @@ def tile_moe_pln_glu_sigmoid_kernel(
                 )
             copy(out=y_sb[n][:, lo * C : hi * C], in_=y_ps)
 
-        gather(0, 2)
-        for lo in range(2, E, 2):
-            gather(lo, 1)
-        for e in range(2):
+        gather(PAIRS[0], ((ORDER[0], 1), (ORDER[1], 1)))
+        for pair in PAIRS[1:]:
+            gather(pair, ((pair[0], 2),))
+        for e in ORDER[:2]:
             sigmoid_of(e)
-        for e in range(2):
+        for e in ORDER[:2]:
             linear_of(e)
-        for e in range(2, 6):
+        for e in ORDER[2:6]:
             sigmoid_of(e)
-        for e in range(2, 4):
+        for e in ORDER[2:4]:
             linear_of(e)
-        for e in range(6, E):
+        for e in ORDER[6:]:
             sigmoid_of(e)
-        for e in range(4, 6):
+        for e in ORDER[4:6]:
             linear_of(e)
-        for e in range(E):
+        for at, e in enumerate(ORDER):
             product(e)
-            if e < 2:
-                linear_of(e + 6)
+            if at < 2:
+                linear_of(ORDER[at + 6])
         for group, at in zip(GROUPS[:3], (2, 3, 6)):
             turn_h(group, bank[at])
         for i in range(KEEP_WARM):
@@ -264,69 +271,64 @@ def tile_moe_pln_glu_sigmoid_kernel(
             turn_h(group, bank[at])
         for group in GROUPS:
             quantise_h(group)
-        second_layer(0, 1, 5, bank[1], nc.vector.tensor_copy)
-        second_layer(0, 0, 1, bank[3], nc.scalar.copy)
-        second_layer(0, 5, 7, bank[2], nc.scalar.copy)
-        second_layer(0, 7, E, bank[4], nc.scalar.copy)
-        second_layer(1, 0, QUAD, bank[5], nc.scalar.copy)
+        second_layer(0, 0, QUAD, bank[1], nc.scalar.copy)
+        second_layer(1, 0, QUAD, bank[2], nc.scalar.copy)
+        second_layer(0, QUAD, E, bank[3], nc.vector.tensor_copy)
         second_layer(1, QUAD, E, bank[6], nc.scalar.copy)
-        second_layer(2, 0, QUAD, bank[7], nc.scalar.copy)
-        second_layer(2, QUAD, E, bank[0], nc.scalar.copy)
+        second_layer(2, 0, QUAD, bank[5], nc.scalar.copy)
+        second_layer(2, QUAD, E, bank[7], nc.scalar.copy)
 
-        parts = {}
+        first = keep.tile([P, NT, T], F32, name="first")
+        second0 = keep.tile([P, T], F32, name="second0")
 
-        def pick(n, which, lo, hi):
-            if (n, which) not in parts:
-                parts[n, which] = keep.tile([P, T], F32, name=f"part{n}{which}")
+        def pick(dst, n, which, lo, hi):
             pos = (pos1_sb, pos2_sb)[which]
             nc.vector.tensor_tensor(
-                parts[n, which][:, lo:hi], y_sb[n][:].indirect(pos[:, lo // 16 : hi // 16]), gates[:, which, lo:hi], MULT
+                dst[:, lo:hi], y_sb[n][:].indirect(pos[:, lo // 16 : hi // 16]), gates[:, which, lo:hi], MULT
             )
 
-        def store(n, lo, hi):
-            result = work.tile([P, hi - lo], F32, name=f"result{hi - lo}")
-            nc.vector.tensor_tensor(result[:], parts[n, 0][:, lo:hi], parts[n, 1][:, lo:hi], ADD)
-            nc.sync.dma_start(out=out[n * P : (n + 1) * P, lo:hi], in_=result[:])
+        pick(first[:, 0, :], 0, 0, 0, T)
+        for lo in range(0, T, HALF):
+            pick(second0, 0, 1, lo, lo + HALF)
+        for lo in range(0, T, HALF):
+            result = work.tile([P, HALF], F32, name="result0")
+            nc.vector.tensor_tensor(result[:], first[:, 0, lo : lo + HALF], second0[:, lo : lo + HALF], ADD)
+            nc.sync.dma_start(out=out[:P, lo : lo + HALF], in_=result[:])
+        for n in range(1, NT):
+            pick(first[:, n, :], n, 0, 0, T)
 
-        def turn_part(n, which, lo, hi, ps):
-            for at in range(0, hi - lo, P):
-                nc.tensor.matmul(
-                    ps[:, at : at + P],
-                    lhsT=parts[n, which][:, lo + at : lo + at + P],
-                    rhs=ident[:],
-                    is_transpose=True,
-                    start=which == 0 and at == 0,
-                    stop=which == 1 and at + P == hi - lo,
-                )
+        def fetch(n, lo, by_token):
+            plain = keep.tile([P, HALF], F32, name="plain", bufs=2)
+            nc.scalar.activation(plain[:], y_sb[n][:].indirect(pos2_sb[:, lo // 16 : (lo + HALF) // 16]), COPY)
+            for b in range(2):
+                nc.tensor.transpose(by_token[b], plain[:, b * P : (b + 1) * P], ident[:])
 
-        def turn_back(width, ps, by_row):
-            summed = work.tile([P, width], F32, name=f"summed{width}")
-            nc.scalar.copy(out=summed[:], in_=ps[:, :width])
-            for at in range(0, width, P):
-                nc.tensor.transpose(by_row[:, at : at + P], summed[:, at : at + P], ident[:])
+        def scale(lo, by_token, by_row):
+            scaled = keep.tile([P, len(by_row) * P], F32, name=f"scaled{lo}_{len(scaled_names)}")
+            scaled_names.append(lo)
+            nc.scalar.activation(scaled[:], by_token, COPY, scale=gate_col[:, lo // P : lo // P + 1])
+            for at, block in enumerate(by_row):
+                nc.tensor.transpose(block, scaled[:, at * P : (at + 1) * P], ident[:])
 
-        def leave(n, lo, by_row):
-            result = work.tile([P, HALF], F32, name="turned_back")
-            nc.scalar.copy(out=result[:], in_=by_row[:, :HALF])
-            nc.scalar.dma_start(out=out[n * P : (n + 1) * P, lo : lo + HALF], in_=result[:])
+        scaled_names = []
 
-        for n, lo, ps, by_row in ((0, 0, bank[5], bank[2]), (0, HALF, bank[6], bank[3]), (1, 0, bank[5], bank[1])):
-            for which in range(2):
-                pick(n, which, lo, lo + HALF)
-            for which in range(2):
-                turn_part(n, which, lo, lo + HALF, ps)
-            turn_back(HALF, ps, by_row)
-            leave(n, lo, by_row)
-        last_blocks = ((HALF, bank[6]), (HALF + P, bank[2]))
-        for which in range(2):
-            pick(1, which, HALF, T)
-            for lo, ps in last_blocks:
-                turn_part(1, which, lo, lo + P, ps)
-        for lo, ps in last_blocks:
-            turn_back(P, ps, bank[3][:, lo - HALF : lo - HALF + P])
-        leave(1, HALF, bank[3])
-        pick(NT - 1, 0, 0, T)
-        pick(NT - 1, 1, 0, HALF)
-        pick(NT - 1, 1, HALF, T)
-        store(NT - 1, 0, HALF)
-        store(NT - 1, HALF, T)
+        def blk(ps, at):
+            return ps[:, at * P : (at + 1) * P]
+
+        fetch(1, 0, (blk(bank[1], 0), blk(bank[3], 0)))
+        fetch(2, 0, (blk(bank[1], 1), blk(bank[3], 1)))
+        fetch(1, HALF, (blk(bank[2], 0), blk(bank[2], 1)))
+        scale(0, bank[1][:, : 2 * P], (blk(bank[4], 0), blk(bank[4], 2)))
+        fetch(2, HALF, (blk(bank[5], 0), blk(bank[6], 0)))
+        scale(P, bank[3][:, : 2 * P], (blk(bank[4], 1), blk(bank[4], 3)))
+        result = keep.tile([P, 2, HALF], F32, name="result_a")
+        nc.vector.tensor_tensor(result[:], bank[4][:].rearrange("p (n t) -> p n t", n=2), first[:, 1:, :HALF], ADD)
+        nc.sync.dma_start(out=out[P:, :HALF].rearrange("(n p) t -> p n t", p=P), in_=result[:])
+        for b in range(2):
+            scale(HALF + b * P, blk(bank[2], b), (blk(bank[7], b),))
+        scale(HALF, blk(bank[5], 0), (blk(bank[0], 0),))
+        scale(HALF + P, blk(bank[6], 0), (blk(bank[0], 1),))
+        for n, ps, queue in ((1, bank[7], nc.sync), (2, bank[0], nc.scalar)):
+            last = keep.tile([P, HALF], F32, name=f"result_b{n}")
+            nc.vector.tensor_tensor(last[:], ps[:, :HALF], first[:, n, HALF:], ADD)
+            queue.dma_start(out=out[n * P : (n + 1) * P, HALF:], in_=last[:])

@@ -7,6 +7,7 @@ P = 128
 T, E, C, K, H, N = 512, 8, 128, 512, 512, 384
 NT = N // P
 HALF = T // 2
+BLOCKS = T // P
 FLOPS = 2 * E * C * (2 * K * H + H * N)
 
 F32 = mybir.dt.float32
@@ -100,29 +101,20 @@ def tile_moe_pln_glu_sigmoid_kernel(
         load_words("w3", w3_words, PAIRS[2])
         load_words("w3", w3_words, PAIRS[3])
         load_scales(planes["w2"], w2_scales)
-        w2_of = {}
-
-        def load_w2(first, last):
-            width = 2 * P * (last - first)
-            tile = keep.tile([P, E * width], U8, name=f"w2_{first}", align_bytes=64)
-            nc.sync.dma_start(
-                out=tile[:].bitcast(I32).rearrange("p (e n) -> p e n", e=E),
-                in_=w2_words[:, 0, :, 2 * P * first : 2 * P * last].rearrange("e p n -> p e n").bitcast(I32),
-            )
-            for e in range(E):
-                for n in range(first, last):
-                    at = e * width + 2 * P * (n - first)
-                    w2_of[e, n] = tile[:, at : at + 2 * P]
-
-        load_w2(0, 1)
+        w2_sb = keep.tile([P, E * 2 * N], U8, name="w2_sb", align_bytes=64)
+        nc.sync.dma_start(
+            out=w2_sb[:].bitcast(I32).rearrange("p (e n) -> p e n", e=E),
+            in_=w2_words[:, 0].rearrange("e p n -> p e n").bitcast(I32),
+        )
+        w2_of = {(e, n): w2_sb[:, 2 * (e * N + n * P) : 2 * (e * N + (n + 1) * P)] for e in range(E) for n in range(NT)}
+        gates = [keep.tile([P, T], F32, name=f"gate{g}") for g in range(2)]
         nc.sync.dma_start(pos1_sb[:], pos1)
+        nc.sync.dma_start(out=gates[0][:], in_=gate[0, :P, :])
         nc.sync.dma_start(pos2_sb[:], pos2)
-        gates = keep.tile([P, 2, T], F32, name="gates")
-        nc.sync.dma_start(out=gates[:], in_=gate[:, :P, :].rearrange("g p t -> p g t"))
-        load_w2(1, NT)
-        gate_col = keep.tile([P, T // P], F32, name="gate_col")
-        with nc.allow_non_contiguous_dma(reason="one gate value a partition"):
-            nc.sync.dma_start(out=gate_col[:], in_=gate[1, 0, :].rearrange("(b p) -> p b", p=P))
+        nc.sync.dma_start(out=gates[1][:], in_=gate[1, :P, :])
+        gate_rows = keep.tile([P, P], F32, name="gate_rows")
+        nc.gpsimd.memset(gate_rows[:], 0.0)
+        nc.sync.dma_start(out=gate_rows[:BLOCKS, :], in_=gate[1, 0, :].rearrange("(b t) -> b t", t=P))
 
         for i in range(2):
             src = x_raw[i][:].rearrange("p j t -> p t j")
@@ -284,7 +276,7 @@ def tile_moe_pln_glu_sigmoid_kernel(
         def pick(dst, n, which, lo, hi):
             pos = (pos1_sb, pos2_sb)[which]
             nc.vector.tensor_tensor(
-                dst[:, lo:hi], y_sb[n][:].indirect(pos[:, lo // 16 : hi // 16]), gates[:, which, lo:hi], MULT
+                dst[:, lo:hi], y_sb[n][:].indirect(pos[:, lo // 16 : hi // 16]), gates[which][:, lo:hi], MULT
             )
 
         pick(first[:, 0, :], 0, 0, 0, T)
@@ -316,6 +308,9 @@ def tile_moe_pln_glu_sigmoid_kernel(
             return ps[:, at * P : (at + 1) * P]
 
         fetch(1, 0, (blk(bank[1], 0), blk(bank[3], 0)))
+        nc.tensor.transpose(blk(bank[7], 0), gate_rows[:], ident[:])
+        gate_col = keep.tile([P, BLOCKS], F32, name="gate_col")
+        nc.scalar.copy(out=gate_col[:], in_=bank[7][:, :BLOCKS])
         fetch(2, 0, (blk(bank[1], 1), blk(bank[3], 1)))
         fetch(1, HALF, (blk(bank[2], 0), blk(bank[2], 1)))
         scale(0, bank[1][:, : 2 * P], (blk(bank[4], 0), blk(bank[4], 2)))

@@ -101,15 +101,26 @@ def tile_moe_pln_glu_sigmoid_kernel(
         load_words("w3", w3_words, PAIRS[2])
         load_words("w3", w3_words, PAIRS[3])
         load_scales(planes["w2"], w2_scales)
-        w2_sb = keep.tile([P, E * 2 * N], U8, name="w2_sb", align_bytes=64)
-        nc.sync.dma_start(
-            out=w2_sb[:].bitcast(I32).rearrange("p (e n) -> p e n", e=E),
-            in_=w2_words[:, 0].rearrange("e p n -> p e n").bitcast(I32),
-        )
-        w2_of = {(e, n): w2_sb[:, 2 * (e * N + n * P) : 2 * (e * N + (n + 1) * P)] for e in range(E) for n in range(NT)}
+        w2_of = {}
+
+        def load_w2(lo, hi, first, last):
+            width = 2 * P * (last - first)
+            tile = keep.tile([P, (hi - lo) * width], U8, name=f"w2_{lo}_{first}", align_bytes=64)
+            nc.sync.dma_start(
+                out=tile[:].bitcast(I32).rearrange("p (e n) -> p e n", e=hi - lo),
+                in_=w2_words[lo:hi, 0, :, 2 * P * first : 2 * P * last].rearrange("e p n -> p e n").bitcast(I32),
+            )
+            for e in range(lo, hi):
+                for n in range(first, last):
+                    at = (e - lo) * width + 2 * P * (n - first)
+                    w2_of[e, n] = tile[:, at : at + 2 * P]
+
         gates = [keep.tile([P, T], F32, name=f"gate{g}") for g in range(2)]
+        load_w2(0, QUAD, 0, NT)
+        load_w2(QUAD, E, 0, 1)
         nc.sync.dma_start(pos1_sb[:], pos1)
         nc.sync.dma_start(out=gates[0][:], in_=gate[0, :P, :])
+        load_w2(QUAD, E, 1, NT)
         nc.sync.dma_start(pos2_sb[:], pos2)
         nc.sync.dma_start(out=gates[1][:], in_=gate[1, :P, :])
         gate_rows = keep.tile([P, P], F32, name="gate_rows")
@@ -266,8 +277,8 @@ def tile_moe_pln_glu_sigmoid_kernel(
         second_layer(0, 0, QUAD, bank[1], nc.scalar.copy)
         second_layer(1, 0, QUAD, bank[2], nc.scalar.copy)
         second_layer(0, QUAD, E, bank[3], nc.vector.tensor_copy)
+        second_layer(2, 0, QUAD, bank[1], nc.scalar.copy)
         second_layer(1, QUAD, E, bank[6], nc.scalar.copy)
-        second_layer(2, 0, QUAD, bank[5], nc.scalar.copy)
         second_layer(2, QUAD, E, bank[7], nc.scalar.copy)
 
         first = keep.tile([P, NT, T], F32, name="first")

@@ -56,6 +56,9 @@ def tile_moe_pln_glu_sigmoid_kernel(
         for i in range(2):
             nc.sync.dma_start(out=x_raw[i][:], in_=xv[:, 2 * i : 2 * i + 2, :])
         nc.sync.dma_start(offs_sb[:], offs)
+        gate_rows = keep.tile([P, P], F32, name="gate_rows")
+        nc.gpsimd.memset(gate_rows[:], 0.0)
+        nc.sync.dma_start(out=gate_rows[:BLOCKS, :], in_=gate[1, 0, :].rearrange("(b t) -> b t", t=P))
 
         def load_scales(plane, src):
             for r in range(4):
@@ -116,16 +119,11 @@ def tile_moe_pln_glu_sigmoid_kernel(
                     w2_of[e, n] = tile[:, at : at + 2 * P]
 
         gates = [keep.tile([P, T], F32, name=f"gate{g}") for g in range(2)]
-        load_w2(0, QUAD, 0, NT)
-        load_w2(QUAD, E, 0, 1)
         nc.sync.dma_start(pos1_sb[:], pos1)
-        nc.sync.dma_start(out=gates[0][:], in_=gate[0, :P, :])
-        load_w2(QUAD, E, 1, NT)
         nc.sync.dma_start(pos2_sb[:], pos2)
+        load_w2(0, E, 0, NT)
+        nc.sync.dma_start(out=gates[0][:], in_=gate[0, :P, :])
         nc.sync.dma_start(out=gates[1][:], in_=gate[1, :P, :])
-        gate_rows = keep.tile([P, P], F32, name="gate_rows")
-        nc.gpsimd.memset(gate_rows[:], 0.0)
-        nc.sync.dma_start(out=gate_rows[:BLOCKS, :], in_=gate[1, 0, :].rearrange("(b t) -> b t", t=P))
 
         for i in range(2):
             src = x_raw[i][:].rearrange("p j t -> p t j")
@@ -139,6 +137,10 @@ def tile_moe_pln_glu_sigmoid_kernel(
                 scales=x_bytes[:, i * HALF : (i + 1) * HALF],
                 in_=x_grp[i][:].rearrange("p t j -> p (t j)"),
             )
+
+        nc.tensor.transpose(bank[7][:, :P], gate_rows[:], ident[:])
+        gate_col = keep.tile([P, BLOCKS], F32, name="gate_col")
+        nc.scalar.copy(out=gate_col[:], in_=bank[7][:, :BLOCKS])
 
         tok_words, tok_bytes = {}, {}
 
@@ -275,66 +277,67 @@ def tile_moe_pln_glu_sigmoid_kernel(
         for group in GROUPS:
             quantise_h(group)
         second_layer(0, 0, QUAD, bank[1], nc.scalar.copy)
+        second_layer(0, QUAD, E - 1, bank[3], nc.vector.tensor_copy)
         second_layer(1, 0, QUAD, bank[2], nc.scalar.copy)
-        second_layer(0, QUAD, E, bank[3], nc.vector.tensor_copy)
-        second_layer(2, 0, QUAD, bank[1], nc.scalar.copy)
+        second_layer(0, E - 1, E, bank[4], nc.vector.tensor_copy)
         second_layer(1, QUAD, E, bank[6], nc.scalar.copy)
-        second_layer(2, QUAD, E, bank[7], nc.scalar.copy)
 
-        first = keep.tile([P, NT, T], F32, name="first")
+        first = {n: keep.tile([P, T], F32, name=f"first{n}") for n in range(NT - 1)}
         second0 = keep.tile([P, T], F32, name="second0")
 
         def pick(dst, n, which, lo, hi):
             pos = (pos1_sb, pos2_sb)[which]
             nc.vector.tensor_tensor(
-                dst[:, lo:hi], y_sb[n][:].indirect(pos[:, lo // 16 : hi // 16]), gates[which][:, lo:hi], MULT
+                dst, y_sb[n][:].indirect(pos[:, lo // 16 : hi // 16]), gates[which][:, lo:hi], MULT
             )
 
-        pick(first[:, 0, :], 0, 0, 0, T)
+        pick(first[0][:], 0, 0, 0, T)
         for lo in range(0, T, HALF):
-            pick(second0, 0, 1, lo, lo + HALF)
-        for lo in range(0, T, HALF):
+            pick(second0[:, lo : lo + HALF], 0, 1, lo, lo + HALF)
+
+        def add_band0(lo):
             result = work.tile([P, HALF], F32, name="result0")
-            nc.vector.tensor_tensor(result[:], first[:, 0, lo : lo + HALF], second0[:, lo : lo + HALF], ADD)
+            nc.vector.tensor_tensor(result[:], first[0][:, lo : lo + HALF], second0[:, lo : lo + HALF], ADD)
             nc.sync.dma_start(out=out[:P, lo : lo + HALF], in_=result[:])
-        for n in range(1, NT):
-            pick(first[:, n, :], n, 0, 0, T)
+
+        add_band0(0)
+
+        def blk(ps, at):
+            return ps[:, at * P : (at + 1) * P]
 
         def fetch(n, lo, by_token):
             plain = keep.tile([P, HALF], F32, name="plain", bufs=2)
             nc.scalar.activation(plain[:], y_sb[n][:].indirect(pos2_sb[:, lo // 16 : (lo + HALF) // 16]), COPY)
             for b in range(2):
-                nc.tensor.transpose(by_token[b], plain[:, b * P : (b + 1) * P], ident[:])
+                nc.tensor.transpose(blk(by_token, b), blk(plain, b), ident[:])
 
-        def scale(lo, by_token, by_row):
-            scaled = keep.tile([P, len(by_row) * P], F32, name=f"scaled{lo}_{len(scaled_names)}")
-            scaled_names.append(lo)
-            nc.scalar.activation(scaled[:], by_token, COPY, scale=gate_col[:, lo // P : lo // P + 1])
-            for at, block in enumerate(by_row):
-                nc.tensor.transpose(block, scaled[:, at * P : (at + 1) * P], ident[:])
+        def scale(n, lo, by_token, by_row):
+            for b in range(2):
+                at = lo // P + b
+                scaled = keep.tile([P, P], F32, name="scaled", tag=f"scaled{n}{at}")
+                nc.scalar.activation(scaled[:], blk(by_token, b), COPY, scale=gate_col[:, at : at + 1])
+                nc.tensor.transpose(by_row[:, b * P : (b + 1) * P], scaled[:], ident[:])
 
-        scaled_names = []
+        def add_and_store(n, lo, hi, by_row, queue):
+            result = keep.tile([P, hi - lo], F32, name=f"result{n}{lo}")
+            nc.vector.tensor_tensor(result[:], by_row, first[n][:, lo:hi], ADD)
+            queue.dma_start(out=out[n * P : (n + 1) * P, lo:hi], in_=result[:])
 
-        def blk(ps, at):
-            return ps[:, at * P : (at + 1) * P]
-
-        fetch(1, 0, (blk(bank[1], 0), blk(bank[3], 0)))
-        nc.tensor.transpose(blk(bank[7], 0), gate_rows[:], ident[:])
-        gate_col = keep.tile([P, BLOCKS], F32, name="gate_col")
-        nc.scalar.copy(out=gate_col[:], in_=bank[7][:, :BLOCKS])
-        fetch(2, 0, (blk(bank[1], 1), blk(bank[3], 1)))
-        fetch(1, HALF, (blk(bank[2], 0), blk(bank[2], 1)))
-        scale(0, bank[1][:, : 2 * P], (blk(bank[4], 0), blk(bank[4], 2)))
-        fetch(2, HALF, (blk(bank[5], 0), blk(bank[6], 0)))
-        scale(P, bank[3][:, : 2 * P], (blk(bank[4], 1), blk(bank[4], 3)))
-        result = keep.tile([P, 2, HALF], F32, name="result_a")
-        nc.vector.tensor_tensor(result[:], bank[4][:].rearrange("p (n t) -> p n t", n=2), first[:, 1:, :HALF], ADD)
-        nc.sync.dma_start(out=out[P:, :HALF].rearrange("(n p) t -> p n t", p=P), in_=result[:])
-        for b in range(2):
-            scale(HALF + b * P, blk(bank[2], b), (blk(bank[7], b),))
-        scale(HALF, blk(bank[5], 0), (blk(bank[0], 0),))
-        scale(HALF + P, blk(bank[6], 0), (blk(bank[0], 1),))
-        for n, ps, queue in ((1, bank[7], nc.sync), (2, bank[0], nc.scalar)):
-            last = keep.tile([P, HALF], F32, name=f"result_b{n}")
-            nc.vector.tensor_tensor(last[:], ps[:, :HALF], first[:, n, HALF:], ADD)
-            queue.dma_start(out=out[n * P : (n + 1) * P, HALF:], in_=last[:])
+        fetch(1, 0, bank[3])
+        fetch(1, HALF, bank[2])
+        second_layer(2, 0, QUAD, bank[1], nc.scalar.copy)
+        pick(first[1][:], 1, 0, 0, T)
+        add_band0(HALF)
+        scale(1, 0, bank[3], bank[4][:, :HALF])
+        scale(1, HALF, bank[2], bank[4][:, HALF:])
+        second_layer(2, QUAD, E, bank[7], nc.scalar.copy)
+        add_and_store(1, 0, T, bank[4][:], nc.sync)
+        fetch(2, 0, bank[5])
+        fetch(2, HALF, bank[6])
+        first[2] = keep.tile([P, T], F32, name="first2", tag="scaled13")
+        for lo in range(0, T, HALF):
+            pick(first[2][:, lo : lo + HALF], 2, 0, lo, lo + HALF)
+        scale(2, 0, bank[5], bank[0][:, :HALF])
+        scale(2, HALF, bank[6], bank[1][:, :HALF])
+        add_and_store(2, 0, HALF, bank[0][:, :HALF], nc.sync)
+        add_and_store(2, HALF, T, bank[1][:, :HALF], nc.scalar)

@@ -291,7 +291,8 @@ def tile_moe_pln_glu_sigmoid_kernel(
                 dst, y_sb[n][:].indirect(pos[:, lo // 16 : hi // 16]), gates[which][:, lo:hi], MULT
             )
 
-        pick(first[0][:], 0, 0, 0, T)
+        for lo in range(0, T, HALF):
+            pick(first[0][:, lo : lo + HALF], 0, 0, lo, lo + HALF)
         for lo in range(0, T, HALF):
             pick(second0[:, lo : lo + HALF], 0, 1, lo, lo + HALF)
 
@@ -326,7 +327,8 @@ def tile_moe_pln_glu_sigmoid_kernel(
         fetch(1, 0, bank[3])
         fetch(1, HALF, bank[2])
         second_layer(2, 0, QUAD, bank[1], nc.scalar.copy)
-        pick(first[1][:], 1, 0, 0, T)
+        for lo in range(0, T, HALF):
+            pick(first[1][:, lo : lo + HALF], 1, 0, lo, lo + HALF)
         add_band0(HALF)
         scale(1, 0, bank[3], bank[4][:, :HALF])
         scale(1, HALF, bank[2], bank[4][:, HALF:])

@@ -8,6 +8,7 @@ T, E, C, K, H, N = 512, 8, 128, 512, 512, 384
 NT = N // P
 HALF = T // 2
 BLOCKS = T // P
+LAST = T - P
 FLOPS = 2 * E * C * (2 * K * H + H * N)
 
 F32 = mybir.dt.float32
@@ -40,7 +41,6 @@ def tile_moe_pln_glu_sigmoid_kernel(
     nc = tc.nc
     with ExitStack() as ctx:
         keep = ctx.enter_context(tc.tile_pool(name="keep", bufs=1))
-        work = ctx.enter_context(tc.tile_pool(name="work", bufs=3))
         psum = ctx.enter_context(tc.psum_pool(name="psum", bufs=1))
         bank = [psum.tile([P, 512], F32, name=f"bank{i}") for i in range(8)]
 
@@ -276,14 +276,16 @@ def tile_moe_pln_glu_sigmoid_kernel(
             turn_h(group, bank[at])
         for group in GROUPS:
             quantise_h(group)
-        second_layer(0, 0, QUAD, bank[1], nc.scalar.copy)
+        second_layer(0, 0, 2, bank[1], nc.scalar.copy)
+        second_layer(1, 0, 2, bank[2], nc.scalar.copy)
+        second_layer(0, 2, QUAD, bank[5], nc.scalar.copy)
         second_layer(0, QUAD, E - 1, bank[3], nc.vector.tensor_copy)
-        second_layer(1, 0, QUAD, bank[2], nc.scalar.copy)
+        second_layer(1, 2, QUAD, bank[6], nc.scalar.copy)
         second_layer(0, E - 1, E, bank[4], nc.vector.tensor_copy)
-        second_layer(1, QUAD, E, bank[6], nc.scalar.copy)
+        second_layer(1, QUAD, E, bank[7], nc.scalar.copy)
 
         first = {n: keep.tile([P, T], F32, name=f"first{n}") for n in range(NT - 1)}
-        second0 = keep.tile([P, T], F32, name="second0")
+        second0 = keep.tile([P, LAST], F32, name="second0")
 
         def pick(dst, n, which, lo, hi):
             pos = (pos1_sb, pos2_sb)[which]
@@ -293,53 +295,52 @@ def tile_moe_pln_glu_sigmoid_kernel(
 
         for lo in range(0, T, HALF):
             pick(first[0][:, lo : lo + HALF], 0, 0, lo, lo + HALF)
-        for lo in range(0, T, HALF):
-            pick(second0[:, lo : lo + HALF], 0, 1, lo, lo + HALF)
-
-        def add_band0(lo):
-            result = work.tile([P, HALF], F32, name="result0")
-            nc.vector.tensor_tensor(result[:], first[0][:, lo : lo + HALF], second0[:, lo : lo + HALF], ADD)
-            nc.sync.dma_start(out=out[:P, lo : lo + HALF], in_=result[:])
-
-        add_band0(0)
+        pick(second0[:, :HALF], 0, 1, 0, HALF)
+        pick(second0[:, HALF:LAST], 0, 1, HALF, LAST)
 
         def blk(ps, at):
             return ps[:, at * P : (at + 1) * P]
 
         def fetch(n, lo, by_token):
-            plain = keep.tile([P, HALF], F32, name="plain", bufs=2)
-            nc.scalar.activation(plain[:], y_sb[n][:].indirect(pos2_sb[:, lo // 16 : (lo + HALF) // 16]), COPY)
-            for b in range(2):
-                nc.tensor.transpose(blk(by_token, b), blk(plain, b), ident[:])
+            hi = lo + len(by_token) * P
+            plain = keep.tile([P, hi - lo], F32, name="plain", bufs=3)
+            nc.scalar.activation(plain[:], y_sb[n][:].indirect(pos2_sb[:, lo // 16 : hi // 16]), COPY)
+            for b, block in enumerate(by_token):
+                nc.tensor.transpose(block, blk(plain, b), ident[:])
 
-        def scale(n, lo, by_token, by_row):
-            for b in range(2):
-                at = lo // P + b
-                scaled = keep.tile([P, P], F32, name="scaled", tag=f"scaled{n}{at}")
-                nc.scalar.activation(scaled[:], blk(by_token, b), COPY, scale=gate_col[:, at : at + 1])
-                nc.tensor.transpose(by_row[:, b * P : (b + 1) * P], scaled[:], ident[:])
+        def scale(name, at, by_token, by_row):
+            scaled = keep.tile([P, len(by_row) * P], F32, name="scaled", tag=name)
+            nc.scalar.activation(scaled[:], by_token, COPY, scale=gate_col[:, at : at + 1])
+            for b, block in enumerate(by_row):
+                nc.tensor.transpose(block, blk(scaled, b), ident[:])
 
-        def add_and_store(n, lo, hi, by_row, queue):
+        def add_and_store(n, lo, hi, by_row, queue, other=None):
             result = keep.tile([P, hi - lo], F32, name=f"result{n}{lo}")
-            nc.vector.tensor_tensor(result[:], by_row, first[n][:, lo:hi], ADD)
+            nc.vector.tensor_tensor(result[:], by_row, first[n][:, lo:hi] if other is None else other, ADD)
             queue.dma_start(out=out[n * P : (n + 1) * P, lo:hi], in_=result[:])
 
-        fetch(1, 0, bank[3])
-        fetch(1, HALF, bank[2])
+        fetch(0, LAST, (blk(bank[2], 2),))
+        fetch(1, 0, (blk(bank[3], 0), blk(bank[3], 1)))
+        fetch(1, HALF, (blk(bank[2], 0), blk(bank[2], 1)))
         second_layer(2, 0, QUAD, bank[1], nc.scalar.copy)
-        for lo in range(0, T, HALF):
-            pick(first[1][:, lo : lo + HALF], 1, 0, lo, lo + HALF)
-        add_band0(HALF)
-        scale(1, 0, bank[3], bank[4][:, :HALF])
-        scale(1, HALF, bank[2], bank[4][:, HALF:])
-        second_layer(2, QUAD, E, bank[7], nc.scalar.copy)
+        second_layer(2, QUAD, E, bank[5], nc.scalar.copy)
+        pick(first[1][:, :HALF], 1, 0, 0, HALF)
+        add_and_store(0, 0, LAST, second0[:], nc.sync)
+        pick(first[1][:, HALF:], 1, 0, HALF, T)
+        early = keep.tile([P, HALF], F32, name="early")
+        pick(early[:], 2, 0, 0, HALF)
+        scale("scaled10", 0, blk(bank[3], 0), (blk(bank[4], 0),))
+        scale("scaled11", 1, blk(bank[3], 1), (blk(bank[4], 1),))
+        scale("scaled12", 2, blk(bank[2], 0), (blk(bank[4], 2),))
+        scale("scaled13", 3, bank[2][:, P : 3 * P], (blk(bank[0], 0), blk(bank[4], 3))[::-1])
+        add_and_store(0, LAST, T, blk(bank[0], 0), nc.sync)
         add_and_store(1, 0, T, bank[4][:], nc.sync)
-        fetch(2, 0, bank[5])
-        fetch(2, HALF, bank[6])
-        first[2] = keep.tile([P, T], F32, name="first2", tag="scaled13")
-        for lo in range(0, T, HALF):
-            pick(first[2][:, lo : lo + HALF], 2, 0, lo, lo + HALF)
-        scale(2, 0, bank[5], bank[0][:, :HALF])
-        scale(2, HALF, bank[6], bank[1][:, :HALF])
-        add_and_store(2, 0, HALF, bank[0][:, :HALF], nc.sync)
-        add_and_store(2, HALF, T, bank[1][:, :HALF], nc.scalar)
+        fetch(2, 0, (blk(bank[7], 0), blk(bank[7], 1)))
+        fetch(2, HALF, (blk(bank[6], 0),))
+        fetch(2, LAST, (blk(bank[5], 0),))
+        late = keep.tile([P, HALF], F32, name="late", tag="scaled13")
+        pick(late[:], 2, 0, HALF, T)
+        for b, ps in enumerate((blk(bank[7], 0), blk(bank[7], 1), blk(bank[6], 0), blk(bank[5], 0))):
+            scale(f"scaled2{b}", b, ps, (blk(bank[1 + b // 2], b % 2),))
+        add_and_store(2, 0, HALF, bank[1][:, :HALF], nc.sync, early[:])
+        add_and_store(2, HALF, T, bank[2][:, :HALF], nc.scalar, late[:])

from contextlib import ExitStack

import concourse.mybir as mybir
from concourse.masks import make_identity

P = 128
T, E, C, K, H, N = 512, 8, 128, 512, 512, 384
NT = N // P
HALF = T // 2
BLOCKS = T // P
LAST = T - P
FLOPS = 2 * E * C * (2 * K * H + H * N)

F32 = mybir.dt.float32
BF16 = mybir.dt.bfloat16
I32 = mybir.dt.int32
U32 = mybir.dt.uint32
U16 = mybir.dt.uint16
U8 = mybir.dt.uint8
FP8X4 = mybir.dt.float8_e4m3fn_x4
FP4X4 = mybir.dt.float4_e2m1fn_x4
MULT = mybir.AluOpType.mult
ADD = mybir.AluOpType.add
SIGMOID = mybir.ActivationFunctionType.Sigmoid
COPY = mybir.ActivationFunctionType.Copy

VECTOR_CAST = 320
QUAD = 4
KEEP_WARM = 2
ORDER = (5, 0, 1, 2, 3, 4, 6, 7)
PAIRS = ((0, 5), (1, 2), (3, 4), (6, 7))
GROUPS = ((0, 1), (2, 3), (4, 5), (6,), (7,))
A_BANKS = dict(zip(ORDER, (0, 1, 2, 3, 0, 1, 2, 3)))
G_BANKS = dict(zip(ORDER, (4, 5, 6, 7, 0, 1, 4, 5)))
ON_GPSIMD = ORDER[:1]


def tile_moe_pln_glu_sigmoid_kernel(
    tc, xT, w1_words, w1_scales, w3_words, w3_scales, w2_words, w2_scales, gate, offs, pos1, pos2, out
):
    nc = tc.nc
    with ExitStack() as ctx:
        keep = ctx.enter_context(tc.tile_pool(name="keep", bufs=1))
        psum = ctx.enter_context(tc.psum_pool(name="psum", bufs=1))
        bank = [psum.tile([P, 512], F32, name=f"bank{i}") for i in range(8)]

        offs_sb = keep.tile([P, E * C // 16], U16, name="offs_sb")
        pos1_sb = keep.tile([P, T // 16], U16, name="pos1_sb")
        pos2_sb = keep.tile([P, T // 16], U16, name="pos2_sb")

        x_raw = [keep.tile([P, 2, T], F32, name=f"x_raw{i}") for i in range(2)]
        x_grp = [keep.tile([P, HALF, 4], BF16, name=f"x_grp{i}", align_bytes=64) for i in range(2)]
        x_words = keep.tile([P, T], U32, name="x_words", align_bytes=64)
        x_bytes = keep.tile([P, T], U8, name="x_bytes", tag="x_bytes", align_bytes=64)
        xv = xT.rearrange("(p j) t -> p j t", j=4)
        for i in range(2):
            nc.sync.dma_start(out=x_raw[i][:], in_=xv[:, 2 * i : 2 * i + 2, :])
        nc.sync.dma_start(offs_sb[:], offs)
        gate_rows = keep.tile([P, P], F32, name="gate_rows")
        nc.gpsimd.memset(gate_rows[:], 0.0)
        nc.sync.dma_start(out=gate_rows[:BLOCKS, :], in_=gate[1, 0, :].rearrange("(b t) -> b t", t=P))

        def load_scales(plane, src):
            for r in range(4):
                nc.sync.dma_start(
                    out=plane[r:P:32, :].bitcast(I32).rearrange("q (e n) -> q e n", e=E),
                    in_=src[:, 0, r:16:4, :].rearrange("e q n -> q e n").bitcast(I32),
                )

        planes = {}
        for label, width in (("w1", H), ("w3", H), ("w2", N)):
            planes[label] = keep.tile([P, E * width], U8, name=f"{label}_sc", align_bytes=64)
        nc.vector.memset(planes["w1"][:].bitcast(I32), 0)
        nc.vector.memset(planes["w3"][:].bitcast(I32), 0)
        nc.vector.memset(x_bytes[:].bitcast(I32), 0)
        nc.vector.memset(planes["w2"][:].bitcast(I32), 0)
        ident = keep.tile([P, P], F32, name="ident")
        make_identity(nc, ident[:])

        slot_words = {lo: keep.tile([P, 2 * C], U32, name=f"gw{lo}", align_bytes=64) for lo, hi in PAIRS}
        slot_bytes = {lo: keep.tile([P, 2 * C], U8, name=f"gb{lo}", align_bytes=64) for lo, hi in PAIRS}

        words_of = {}

        def load_words(label, words, pair):
            lo, hi = pair
            width = words.shape[3]
            tile = keep.tile([P, 2 * width], U8, name=f"{label}_{lo}", align_bytes=64)
            nc.sync.dma_start(
                out=tile[:].bitcast(I32).rearrange("p (e n) -> p e n", e=2),
                in_=words[lo : hi + 1 : hi - lo, 0].rearrange("e p n -> p e n").bitcast(I32),
            )
            for at, e in enumerate(pair):
                words_of[label, e] = tile[:, at * width : (at + 1) * width]

        load_words("w1", w1_words, PAIRS[0])
        load_scales(planes["w1"], w1_scales)
        load_scales(planes["w3"], w3_scales)
        load_words("w3", w3_words, PAIRS[0])
        load_words("w1", w1_words, PAIRS[1])
        load_words("w1", w1_words, PAIRS[2])
        load_words("w3", w3_words, PAIRS[1])
        load_words("w1", w1_words, PAIRS[3])
        load_words("w3", w3_words, PAIRS[2])
        load_words("w3", w3_words, PAIRS[3])
        load_scales(planes["w2"], w2_scales)
        w2_of = {}

        def load_w2(lo, hi, first, last):
            width = 2 * P * (last - first)
            tile = keep.tile([P, (hi - lo) * width], U8, name=f"w2_{lo}_{first}", align_bytes=64)
            nc.sync.dma_start(
                out=tile[:].bitcast(I32).rearrange("p (e n) -> p e n", e=hi - lo),
                in_=w2_words[lo:hi, 0, :, 2 * P * first : 2 * P * last].rearrange("e p n -> p e n").bitcast(I32),
            )
            for e in range(lo, hi):
                for n in range(first, last):
                    at = (e - lo) * width + 2 * P * (n - first)
                    w2_of[e, n] = tile[:, at : at + 2 * P]

        gates = [keep.tile([P, T], F32, name=f"gate{g}") for g in range(2)]
        nc.sync.dma_start(pos1_sb[:], pos1)
        nc.sync.dma_start(pos2_sb[:], pos2)
        load_w2(0, E, 0, NT)
        nc.sync.dma_start(out=gates[0][:], in_=gate[0, :P, :])
        nc.sync.dma_start(out=gates[1][:], in_=gate[1, :P, :])

        for i in range(2):
            src = x_raw[i][:].rearrange("p j t -> p t j")
            pair = slice(2 * i, 2 * i + 2)
            nc.vector.tensor_copy(out=x_grp[0][:, :, pair], in_=src[:, :HALF, :])
            nc.vector.tensor_copy(out=x_grp[1][:, : VECTOR_CAST - HALF, pair], in_=src[:, HALF:VECTOR_CAST, :])
            nc.scalar.copy(out=x_grp[1][:, VECTOR_CAST - HALF :, pair], in_=src[:, VECTOR_CAST:, :])
        for i in range(2):
            nc.vector.quantize_mx(
                out=x_words[:, i * HALF : (i + 1) * HALF].bitcast(FP8X4),
                scales=x_bytes[:, i * HALF : (i + 1) * HALF],
                in_=x_grp[i][:].rearrange("p t j -> p (t j)"),
            )

        nc.tensor.transpose(bank[7][:, :P], gate_rows[:], ident[:])
        gate_col = keep.tile([P, BLOCKS], F32, name="gate_col")
        nc.scalar.copy(out=gate_col[:], in_=bank[7][:, :BLOCKS])

        tok_words, tok_bytes = {}, {}

        def gather(pair, runs):
            gw, gb = slot_words[pair[0]], slot_bytes[pair[0]]
            for first_e, count in runs:
                at = pair.index(first_e) * C
                part = offs_sb[:, first_e * C // 16 : (first_e + count) * C // 16]
                nc.vector.tensor_copy(gw[:, at : at + count * C], x_words[:].indirect(part))
                nc.vector.tensor_copy(gb[:, at : at + count * C], x_bytes[:].indirect(part))
            for at, e in enumerate(pair):
                tok_words[e] = gw[:, at * C : (at + 1) * C]
                tok_bytes[e] = gb[:, at * C : (at + 1) * C]

        y_sb = [keep.tile([P, E * C], F32, name=f"y_sb{n}") for n in range(NT)]
        live = {}

        sigs = {}

        def first_pass(ps, label, e):
            nc.tensor.matmul_mx(
                out=ps[:],
                lhsT=tok_words[e].bitcast(FP8X4),
                lhsT_scale=tok_bytes[e],
                rhs=words_of[label, e].bitcast(FP4X4),
                rhs_scale=planes[label][:, e * H : (e + 1) * H],
                start=True,
                stop=True,
            )

        def sigmoid_of(e):
            a_ps = bank[A_BANKS[e]]
            first_pass(a_ps, "w1", e)
            sigs[e] = keep.tile([C, H], F32, name=f"sig{e}")
            nc.scalar.activation(
                sigs[e][:].rearrange("c (u m d) -> c u m d", u=2, d=2),
                a_ps[:].rearrange("c (m u d) -> c u m d", u=2, d=2),
                SIGMOID,
            )

        def linear_of(e):
            g_ps = bank[G_BANKS[e]]
            first_pass(g_ps, "w3", e)
            live[e] = g_ps
            if e in ON_GPSIMD:
                g_sb = keep.tile([C, H], F32, name=f"g_sb{e}")
                nc.scalar.copy(
                    out=g_sb[:].rearrange("c (u m d) -> c u m d", u=2, d=2),
                    in_=g_ps[:].rearrange("c (m u d) -> c u m d", u=2, d=2),
                )
                live[e] = g_sb

        def product(e):
            sig, g_ps = sigs[e], live[e]
            if e in ON_GPSIMD:
                held = "x_bytes" if e == ON_GPSIMD[0] else f"h_row{e}"
                h_row = keep.tile([C, H], BF16, name=f"h_row{e}", tag=held, align_bytes=64)
                nc.gpsimd.tensor_tensor(h_row[:], sig[:], g_ps[:], MULT)
                live[e] = h_row
                return
            h_row = keep.tile([C, H], BF16, name=f"h_row{e}", align_bytes=64)
            nc.vector.tensor_tensor(
                h_row[:].rearrange("c (u m d) -> c u m d", u=2, d=2),
                sig[:].rearrange("c (u m d) -> c u m d", u=2, d=2),
                g_ps[:].rearrange("c (m u d) -> c u m d", u=2, d=2),
                MULT,
            )
            live[e] = h_row

        h_grp = {
            group: keep.tile([P, len(group) * C * 4], BF16, name=f"h_grp{group[0]}", align_bytes=64) for group in GROUPS
        }

        def turn_h(group, ps):
            turn = ps[:, : len(group) * 2 * C].rearrange("p (e u c) -> p e u c", u=2, c=C)
            for at, e in enumerate(group):
                h_pairs = live[e][:].bitcast(F32)
                for u in range(2):
                    nc.tensor.transpose(turn[:, at, u, :], h_pairs[:, u * P : (u + 1) * P], ident[:])
            nc.scalar.copy(
                out=h_grp[group][:].bitcast(F32).rearrange("p (e c u) -> p e c u", u=2, c=C),
                in_=turn.rearrange("p e u c -> p e c u"),
            )

        h_words, h_bytes = {}, {}

        def quantise_h(group):
            words = keep.tile([P, len(group) * C], U32, name=f"h_words{group[0]}", align_bytes=64)
            scales = keep.tile([P, len(group) * C], U8, name=f"h_bytes{group[0]}", align_bytes=64)
            nc.vector.quantize_mx(out=words[:].bitcast(FP8X4), scales=scales[:], in_=h_grp[group][:])
            for at, e in enumerate(group):
                h_words[e] = words[:, at * C : (at + 1) * C]
                h_bytes[e] = scales[:, at * C : (at + 1) * C]

        def second_layer(n, lo, hi, ps, copy):
            y_ps = ps[:, : (hi - lo) * C]
            for e in range(lo, hi):
                nc.tensor.matmul_mx(
                    out=y_ps[:, (e - lo) * C : (e - lo + 1) * C],
                    lhsT=w2_of[e, n].bitcast(FP4X4),
                    lhsT_scale=planes["w2"][:, e * N + n * P : e * N + (n + 1) * P],
                    rhs=h_words[e].bitcast(FP8X4),
                    rhs_scale=h_bytes[e],
                    start=True,
                    stop=True,
                )
            copy(out=y_sb[n][:, lo * C : hi * C], in_=y_ps)

        gather(PAIRS[0], ((ORDER[0], 1), (ORDER[1], 1)))
        for pair in PAIRS[1:]:
            gather(pair, ((pair[0], 2),))
        for e in ORDER[:2]:
            sigmoid_of(e)
        for e in ORDER[:2]:
            linear_of(e)
        for e in ORDER[2:6]:
            sigmoid_of(e)
        for e in ORDER[2:4]:
            linear_of(e)
        for e in ORDER[6:]:
            sigmoid_of(e)
        for e in ORDER[4:6]:
            linear_of(e)
        for at, e in enumerate(ORDER):
            product(e)
            if at < 2:
                linear_of(ORDER[at + 6])
        for group, at in zip(GROUPS[:3], (2, 3, 6)):
            turn_h(group, bank[at])
        for i in range(KEEP_WARM):
            first_pass(bank[1], "w3", E - 1)
        for group, at in zip(GROUPS[3:], (7, 0)):
            turn_h(group, bank[at])
        for group in GROUPS:
            quantise_h(group)
        second_layer(0, 0, 2, bank[1], nc.scalar.copy)
        second_layer(1, 0, 2, bank[2], nc.scalar.copy)
        second_layer(0, 2, QUAD, bank[5], nc.scalar.copy)
        second_layer(0, QUAD, E - 1, bank[3], nc.vector.tensor_copy)
        second_layer(1, 2, QUAD, bank[6], nc.scalar.copy)
        second_layer(0, E - 1, E, bank[4], nc.vector.tensor_copy)
        second_layer(1, QUAD, E, bank[7], nc.scalar.copy)

        first = {n: keep.tile([P, T], F32, name=f"first{n}") for n in range(NT - 1)}
        second0 = keep.tile([P, LAST], F32, name="second0")

        def pick(dst, n, which, lo, hi):
            pos = (pos1_sb, pos2_sb)[which]
            nc.vector.tensor_tensor(
                dst, y_sb[n][:].indirect(pos[:, lo // 16 : hi // 16]), gates[which][:, lo:hi], MULT
            )

        for lo in range(0, T, HALF):
            pick(first[0][:, lo : lo + HALF], 0, 0, lo, lo + HALF)
        pick(second0[:, :HALF], 0, 1, 0, HALF)
        pick(second0[:, HALF:LAST], 0, 1, HALF, LAST)

        def blk(ps, at):
            return ps[:, at * P : (at + 1) * P]

        def fetch(n, lo, by_token):
            hi = lo + len(by_token) * P
            plain = keep.tile([P, hi - lo], F32, name="plain", bufs=3)
            nc.scalar.activation(plain[:], y_sb[n][:].indirect(pos2_sb[:, lo // 16 : hi // 16]), COPY)
            for b, block in enumerate(by_token):
                nc.tensor.transpose(block, blk(plain, b), ident[:])

        def scale(name, at, by_token, by_row):
            scaled = keep.tile([P, len(by_row) * P], F32, name="scaled", tag=name)
            nc.scalar.activation(scaled[:], by_token, COPY, scale=gate_col[:, at : at + 1])
            for b, block in enumerate(by_row):
                nc.tensor.transpose(block, blk(scaled, b), ident[:])

        def add_and_store(n, lo, hi, by_row, queue, other=None):
            result = keep.tile([P, hi - lo], F32, name=f"result{n}{lo}")
            nc.vector.tensor_tensor(result[:], by_row, first[n][:, lo:hi] if other is None else other, ADD)
            queue.dma_start(out=out[n * P : (n + 1) * P, lo:hi], in_=result[:])

        fetch(0, LAST, (blk(bank[2], 2),))
        fetch(1, 0, (blk(bank[3], 0), blk(bank[3], 1)))
        fetch(1, HALF, (blk(bank[2], 0), blk(bank[2], 1)))
        second_layer(2, 0, QUAD, bank[1], nc.scalar.copy)
        second_layer(2, QUAD, E, bank[5], nc.scalar.copy)
        pick(first[1][:, :HALF], 1, 0, 0, HALF)
        add_and_store(0, 0, LAST, second0[:], nc.sync)
        pick(first[1][:, HALF:], 1, 0, HALF, T)
        early = keep.tile([P, HALF], F32, name="early")
        pick(early[:], 2, 0, 0, HALF)
        scale("scaled10", 0, blk(bank[3], 0), (blk(bank[4], 0),))
        scale("scaled11", 1, blk(bank[3], 1), (blk(bank[4], 1),))
        scale("scaled12", 2, blk(bank[2], 0), (blk(bank[4], 2),))
        scale("scaled13", 3, bank[2][:, P : 3 * P], (blk(bank[0], 0), blk(bank[4], 3))[::-1])
        add_and_store(0, LAST, T, blk(bank[0], 0), nc.sync)
        add_and_store(1, 0, T, bank[4][:], nc.sync)
        fetch(2, 0, (blk(bank[7], 0), blk(bank[7], 1)))
        fetch(2, HALF, (blk(bank[6], 0),))
        fetch(2, LAST, (blk(bank[5], 0),))
        late = keep.tile([P, HALF], F32, name="late", tag="scaled13")
        pick(late[:], 2, 0, HALF, T)
        for b, ps in enumerate((blk(bank[7], 0), blk(bank[7], 1), blk(bank[6], 0), blk(bank[5], 0))):
            scale(f"scaled2{b}", b, ps, (blk(bank[1 + b // 2], b % 2),))
        add_and_store(2, 0, HALF, bank[1][:, :HALF], nc.sync, early[:])
        add_and_store(2, HALF, T, bank[2][:, :HALF], nc.scalar, late[:])
